import numpy as np
import ml_dtypes


def mxq(x, axis, fmt="e4m3"):
    dtype, down = {"e4m3": (ml_dtypes.float8_e4m3fn, 7), "e5m2": (ml_dtypes.float8_e5m2, 14)}[fmt]
    v = np.moveaxis(np.asarray(x, np.float32).astype(ml_dtypes.bfloat16).astype(np.float64), axis, -1)
    blocks = v.reshape(v.shape[:-1] + (-1, 32))
    amax = np.abs(blocks).max(-1, keepdims=True)
    byte = np.maximum(np.where(amax > 0, np.frexp(amax)[1] - 1 + 127, 0) - down, 1)
    scale = np.exp2(byte - 127.0)
    codes = (blocks / scale).astype(np.float32).astype(dtype).astype(np.float64)
    return np.moveaxis((codes * scale).reshape(v.shape), -1, axis)


WIDE = False


def mx_kscale(k):
    if not WIDE:
        return np.ones(k)
    levels = np.array([10, -10, 5, -5, 0])
    if k % 512:
        return np.exp2(np.random.permutation(np.resize(levels, k // 32))).repeat(32)
    a = np.empty((k // 512, 16))
    for p in range(k // 512):
        a[p, :8] = np.random.permutation(np.resize(levels, 8))
        for g in range(8):
            far = levels[np.abs(levels - a[p, g]) >= 10]
            a[p, g + 8] = far[np.random.randint(len(far))]
    return np.exp2(a.ravel()).repeat(32)


def f64(x):
    return np.asarray(x).astype(np.float64)


def striped(idx):
    return np.tile(np.asarray(idx).reshape(-1, 16).T, (8, 1)).astype(np.uint16)


def unstriped(offs):
    return offs[:16].T.reshape(-1).astype(np.int64)


O, G, T, D, M = 2, 512, 2048, 512, 128


def setup_inputs():
    n = np.random.standard_normal
    s = mx_kscale(D)[:, None]
    grid = lambda x: np.round(x * 32) / 32
    return {
        "cb": (grid(n((O, D, T))) / s).astype(np.float32),
        "w": (n((D, M)) * s / np.sqrt(O * D)).astype(np.float32),
        "norm": np.tile(np.random.randint(32, 129, G) / 64.0, (128, 1)).astype(np.float32),
        "offs": striped(np.random.randint(0, T, O * G)),
    }


def reference(cb, w, norm, offs):
    code = unstriped(offs).reshape(O, G)
    e = sum(f64(cb)[o][:, code[o]] for o in range(O)) * f64(norm)[:1]
    y = mxq(f64(w), 0, "e4m3").T @ mxq(e, 0, "e4m3")
    return y

@@ -1,0 +1,176 @@
+from contextlib import ExitStack
+
+import concourse.mybir as mybir
+from concourse.masks import make_identity
+
+F32 = mybir.dt.float32
+BF16 = mybir.dt.bfloat16
+U32 = mybir.dt.uint32
+U16 = mybir.dt.uint16
+U8 = mybir.dt.uint8
+FP8X4 = mybir.dt.float8_e4m3fn_x4
+MULT = mybir.AluOpType.mult
+ADD = mybir.AluOpType.add
+
+P = 128
+PACK = 4
+BOOKS = 2
+CODEWORDS = 2048
+COLS = 512
+M = 128
+FLOPS = 2 * 512 * COLS * M
+
+CHUNKS = ((0, 128), (128, 256), (256, 384), (384, 448), (448, 512))
+SPLIT = 448
+LAST = PACK - 1
+
+
+def tile_attend_aq_kernel(tc, cb, w, norm, offs, out):
+    nc = tc.nc
+    with ExitStack() as ctx:
+        keep = ctx.enter_context(tc.tile_pool(name="keep", bufs=1))
+        psum = ctx.enter_context(tc.psum_pool(name="psum", bufs=1))
+
+        planes = cb.rearrange("o (p j) c -> o p j c", j=PACK)
+        windows = {}
+
+        def load_window(o, j):
+            windows[o, j] = keep.tile([P, CODEWORDS], F32, name=f"window{o}{j}")
+            nc.sync.dma_start(out=windows[o, j][:], in_=planes[o, :, j, :])
+
+        norm_rows = keep.tile([P, P], F32, name="norm_rows")
+        nc.gpsimd.memset(norm_rows[:], 0.0)
+
+        load_window(0, 0)
+        nc.sync.dma_start(out=norm_rows[0:4, :], in_=norm[0:1, :].rearrange("o (b j) -> (o b) j", b=4))
+        offsets = keep.tile([P, BOOKS * COLS // 16], U16, name="offsets")
+        nc.sync.dma_start(offsets[:], offs)
+        for j in range(PACK):
+            for o in range(BOOKS):
+                if (o, j) != (0, 0):
+                    load_window(o, j)
+        w_raw = keep.tile([P, PACK, M], F32, name="w_raw")
+        nc.sync.dma_start(out=w_raw[:], in_=w.rearrange("(p j) m -> p j m", j=PACK))
+
+        ident = keep.tile([P, P], F32, name="ident")
+        make_identity(nc, ident[:])
+        norm_turned = psum.tile([P, P], F32, name="norm_turned")
+        nc.tensor.transpose(norm_turned[:], norm_rows[:], ident[:])
+        norm_cols = keep.tile([P, 4], F32, name="norm_cols")
+        nc.scalar.copy(out=norm_cols[:], in_=norm_turned[:, 0:4])
+        norm_spread = psum.tile([P, COLS], F32, name="norm_spread")
+        for b in range(4):
+            nc.tensor.transpose(
+                norm_spread[:, b * P : (b + 1) * P], norm_cols[:, b : b + 1].to_broadcast([P, P]), ident[:]
+            )
+        norm_all = keep.tile([P, COLS], F32, name="norm_all")
+        nc.scalar.copy(out=norm_all[:], in_=norm_spread[:])
+
+        e_main = keep.tile([P, SPLIT, PACK], BF16, name="e_main", align_bytes=64)
+        e_last = keep.tile([P, COLS - SPLIT, PACK], BF16, name="e_last", align_bytes=64)
+        e_codes = keep.tile([P, COLS], U32, name="e_codes", align_bytes=64)
+        e_scales = keep.tile([P, COLS], U8, name="e_scales", align_bytes=64)
+        scaled = {}
+        for j in range(PACK):
+            for o in range(BOOKS):
+                scaled[o, j] = keep.tile([P, COLS], F32, name=f"scaled{o}{j}")
+        sums = [keep.tile([P, SPLIT], BF16, name=f"sums{j}") for j in range(PACK)]
+
+        def gather(o, j, lo, hi):
+            first = o * COLS // 16
+            nc.vector.tensor_tensor(
+                scaled[o, j][:, lo:hi],
+                windows[o, j][:].indirect(offsets[:, first + lo // 16 : first + hi // 16]),
+                norm_all[:, lo:hi],
+                MULT,
+            )
+
+        def add(j, lo, hi):
+            if lo >= SPLIT:
+                target = e_last[:, lo - SPLIT : hi - SPLIT, j]
+            else:
+                target = sums[j][:, lo:hi]
+            nc.vector.tensor_tensor(target, scaled[0, j][:, lo:hi], scaled[1, j][:, lo:hi], ADD)
+
+        def interleave(j, lo, hi):
+            nc.scalar.copy(out=e_main[:, lo:hi, j], in_=sums[j][:, lo:hi])
+
+        for j in range(LAST):
+            gather(0, j, 0, COLS)
+            gather(1, j, 0, COLS)
+            add(j, 0, SPLIT)
+            interleave(j, 0, SPLIT)
+            add(j, SPLIT, COLS)
+        gather(0, LAST, 0, COLS)
+
+        w_grouped = keep.tile([P, M, PACK], BF16, name="w_grouped", align_bytes=64)
+        w_codes = keep.tile([P, M], U32, name="w_codes", align_bytes=64)
+        w_scales = keep.tile([P, M], U8, name="w_scales", align_bytes=64)
+        nc.scalar.copy(out=w_grouped[:], in_=w_raw[:].rearrange("p j m -> p m j"))
+
+        def quantise(lo, hi):
+            if lo >= SPLIT:
+                source = e_last[:, lo - SPLIT : hi - SPLIT, :]
+            else:
+                source = e_main[:, lo:hi, :]
+            nc.vector.quantize_mx(
+                out=e_codes[:, lo:hi].bitcast(FP8X4),
+                scales=e_scales[:, lo:hi],
+                in_=source.rearrange("p n j -> p (n j)"),
+            )
+
+        banks = {}
+        for name, lo, hi in (("y0", 0, 256), ("y1", 256, 448), ("y2", 448, 512)):
+            banks[lo, hi] = psum.tile([P, hi - lo], F32, name=name)
+        result = keep.tile([P, COLS], F32, name="result")
+
+        def multiply(lo, hi):
+            for (blo, bhi), bank in banks.items():
+                if blo <= lo and hi <= bhi:
+                    nc.tensor.matmul_mx(
+                        out=bank[:, lo - blo : hi - blo],
+                        lhsT=w_codes[:].bitcast(FP8X4),
+                        lhsT_scale=w_scales[:],
+                        rhs=e_codes[:, lo:hi].bitcast(FP8X4),
+                        rhs_scale=e_scales[:, lo:hi],
+                        start=True,
+                        stop=True,
+                    )
+
+        def finish(lo, hi):
+            if hi == COLS:
+                nc.vector.tensor_copy(out=result[:, lo:hi], in_=banks[lo, hi][:])
+            else:
+                nc.scalar.copy(out=result[:, lo:hi], in_=banks[lo, hi][:])
+            nc.sync.dma_start(out=out[:, lo:hi], in_=result[:, lo:hi])
+
+        gather(1, LAST, *CHUNKS[0])
+        gather(1, LAST, *CHUNKS[1])
+        add(LAST, *CHUNKS[0])
+        interleave(LAST, *CHUNKS[0])
+        gather(1, LAST, *CHUNKS[2])
+        add(LAST, *CHUNKS[1])
+        interleave(LAST, *CHUNKS[1])
+        gather(1, LAST, *CHUNKS[3])
+        add(LAST, *CHUNKS[2])
+        interleave(LAST, *CHUNKS[2])
+        nc.vector.quantize_mx(
+            out=w_codes[:].bitcast(FP8X4), scales=w_scales[:], in_=w_grouped[:].rearrange("p m j -> p (m j)")
+        )
+        gather(1, LAST, *CHUNKS[4])
+        add(LAST, *CHUNKS[3])
+        interleave(LAST, *CHUNKS[3])
+        quantise(*CHUNKS[0])
+        multiply(*CHUNKS[0])
+        add(LAST, *CHUNKS[4])
+        quantise(*CHUNKS[1])
+        multiply(*CHUNKS[1])
+        finish(0, 256)
+        quantise(*CHUNKS[2])
+        multiply(*CHUNKS[2])
+        quantise(*CHUNKS[3])
+        multiply(*CHUNKS[3])
+        finish(256, 448)
+        quantise(*CHUNKS[4])
+        multiply(*CHUNKS[4])
+        finish(448, 512)

@@ -31,24 +31,29 @@ def tile_attend_aq_kernel(tc, cb, w, norm, offs, out):
         keep = ctx.enter_context(tc.tile_pool(name="keep", bufs=1))
         psum = ctx.enter_context(tc.psum_pool(name="psum", bufs=1))
 
-        planes = cb.rearrange("o (p j) c -> o p j c", j=PACK)
+        rows = cb.rearrange("o (p j) c -> o p (j c)", j=PACK)
         windows = {}
+        whole = {}
 
-        def load_window(o, j):
-            windows[o, j] = keep.tile([P, CODEWORDS], F32, name=f"window{o}{j}")
-            nc.sync.dma_start(out=windows[o, j][:], in_=planes[o, :, j, :])
+        def load_planes(o, first, count):
+            tile = keep.tile([P, count * CODEWORDS], F32, name=f"planes{o}{first}")
+            nc.sync.dma_start(out=tile[:], in_=rows[o, :, first * CODEWORDS : (first + count) * CODEWORDS])
+            whole[o, first] = tile[:]
+            for j in range(count):
+                windows[o, first + j] = tile[:, j * CODEWORDS : (j + 1) * CODEWORDS]
 
         norm_rows = keep.tile([P, P], F32, name="norm_rows")
         nc.gpsimd.memset(norm_rows[:], 0.0)
 
-        load_window(0, 0)
+        load_planes(0, 0, 2)
         nc.sync.dma_start(out=norm_rows[0:4, :], in_=norm[0:1, :].rearrange("o (b j) -> (o b) j", b=4))
         offsets = keep.tile([P, BOOKS * COLS // 16], U16, name="offsets")
         nc.sync.dma_start(offsets[:], offs)
-        for j in range(PACK):
-            for o in range(BOOKS):
-                if (o, j) != (0, 0):
-                    load_window(o, j)
+        load_planes(1, 1, 2)
+        load_planes(1, 0, 1)
+        load_planes(0, 2, 1)
+        load_planes(1, LAST, 1)
+        load_planes(0, LAST, 1)
         w_raw = keep.tile([P, PACK, M], F32, name="w_raw")
         nc.sync.dma_start(out=w_raw[:], in_=w.rearrange("(p j) m -> p j m", j=PACK))
 
@@ -70,38 +75,51 @@ def tile_attend_aq_kernel(tc, cb, w, norm, offs, out):
         e_last = keep.tile([P, COLS - SPLIT, PACK], BF16, name="e_last", align_bytes=64)
         e_codes = keep.tile([P, COLS], U32, name="e_codes", align_bytes=64)
         e_scales = keep.tile([P, COLS], U8, name="e_scales", align_bytes=64)
-        scaled = {}
-        for j in range(PACK):
-            for o in range(BOOKS):
-                scaled[o, j] = keep.tile([P, COLS], F32, name=f"scaled{o}{j}")
-        sums = [keep.tile([P, SPLIT], BF16, name=f"sums{j}") for j in range(PACK)]
+        picked = [keep.tile([P, COLS], F32, name=f"picked{j}") for j in range(PACK)]
+        summed = [keep.tile([P, COLS], F32, name=f"summed{j}") for j in range(PACK)]
+        rounded = [keep.tile([P, COLS], BF16, name=f"rounded{j}") for j in range(PACK)]
+
+        def entries(o, lo, hi):
+            first = o * COLS // 16
+            return offsets[:, first + lo // 16 : first + hi // 16]
+
+        def pick(o, j):
+            nc.vector.tensor_copy(picked[j][:], windows[o, j].indirect(entries(o, 0, COLS)))
 
         def gather(o, j, lo, hi):
-            first = o * COLS // 16
             nc.vector.tensor_tensor(
-                scaled[o, j][:, lo:hi],
-                windows[o, j][:].indirect(offsets[:, first + lo // 16 : first + hi // 16]),
-                norm_all[:, lo:hi],
-                MULT,
+                summed[j][:, lo:hi], whole[o, j].indirect(entries(o, lo, hi)), picked[j][:, lo:hi], ADD
             )
 
         def add(j, lo, hi):
-            if lo >= SPLIT:
+            if lo >= SPLIT and j >= 2:
                 target = e_last[:, lo - SPLIT : hi - SPLIT, j]
             else:
-                target = sums[j][:, lo:hi]
-            nc.vector.tensor_tensor(target, scaled[0, j][:, lo:hi], scaled[1, j][:, lo:hi], ADD)
+                target = rounded[j][:, lo:hi]
+            nc.vector.tensor_tensor(target, summed[j][:, lo:hi], norm_all[:, lo:hi], MULT)
 
         def interleave(j, lo, hi):
-            nc.scalar.copy(out=e_main[:, lo:hi, j], in_=sums[j][:, lo:hi])
+            if lo >= SPLIT:
+                nc.scalar.copy(out=e_last[:, lo - SPLIT : hi - SPLIT, j], in_=rounded[j][:, lo:hi])
+            else:
+                nc.scalar.copy(out=e_main[:, lo:hi, j], in_=rounded[j][:, lo:hi])
 
-        for j in range(LAST):
-            gather(0, j, 0, COLS)
-            gather(1, j, 0, COLS)
-            add(j, 0, SPLIT)
-            interleave(j, 0, SPLIT)
-            add(j, SPLIT, COLS)
-        gather(0, LAST, 0, COLS)
+        pick(0, 0)
+        pick(0, 1)
+        gather(1, 1, 0, COLS)
+        pick(1, 2)
+        add(1, 0, COLS)
+        interleave(1, 0, SPLIT)
+        interleave(1, SPLIT, COLS)
+        gather(1, 0, 0, COLS)
+        add(0, 0, COLS)
+        interleave(0, 0, SPLIT)
+        interleave(0, SPLIT, COLS)
+        gather(0, 2, 0, COLS)
+        add(2, 0, SPLIT)
+        interleave(2, 0, SPLIT)
+        add(2, SPLIT, COLS)
+        pick(1, LAST)
 
         w_grouped = keep.tile([P, M, PACK], BF16, name="w_grouped", align_bytes=64)
         w_codes = keep.tile([P, M], U32, name="w_codes", align_bytes=64)
@@ -144,20 +162,20 @@ def tile_attend_aq_kernel(tc, cb, w, norm, offs, out):
                 nc.scalar.copy(out=result[:, lo:hi], in_=banks[lo, hi][:])
             nc.sync.dma_start(out=out[:, lo:hi], in_=result[:, lo:hi])
 
-        gather(1, LAST, *CHUNKS[0])
-        gather(1, LAST, *CHUNKS[1])
+        gather(0, LAST, *CHUNKS[0])
+        gather(0, LAST, *CHUNKS[1])
         add(LAST, *CHUNKS[0])
         interleave(LAST, *CHUNKS[0])
-        gather(1, LAST, *CHUNKS[2])
+        gather(0, LAST, *CHUNKS[2])
         add(LAST, *CHUNKS[1])
         interleave(LAST, *CHUNKS[1])
-        gather(1, LAST, *CHUNKS[3])
+        gather(0, LAST, *CHUNKS[3])
         add(LAST, *CHUNKS[2])
         interleave(LAST, *CHUNKS[2])
         nc.vector.quantize_mx(
             out=w_codes[:].bitcast(FP8X4), scales=w_scales[:], in_=w_grouped[:].rearrange("p m j -> p (m j)")
         )
-        gather(1, LAST, *CHUNKS[4])
+        gather(0, LAST, *CHUNKS[4])
         add(LAST, *CHUNKS[3])
         interleave(LAST, *CHUNKS[3])
         quantise(*CHUNKS[0])

@@ -45,15 +45,14 @@ def tile_attend_aq_kernel(tc, cb, w, norm, offs, out):
         norm_rows = keep.tile([P, P], F32, name="norm_rows")
         nc.gpsimd.memset(norm_rows[:], 0.0)
 
-        load_planes(0, 0, 2)
+        load_planes(0, 0, 1)
         nc.sync.dma_start(out=norm_rows[0:4, :], in_=norm[0:1, :].rearrange("o (b j) -> (o b) j", b=4))
         offsets = keep.tile([P, BOOKS * COLS // 16], U16, name="offsets")
         nc.sync.dma_start(offsets[:], offs)
-        load_planes(1, 1, 2)
         load_planes(1, 0, 1)
-        load_planes(0, 2, 1)
-        load_planes(1, LAST, 1)
-        load_planes(0, LAST, 1)
+        for j in range(1, PACK):
+            load_planes(0, j, 1)
+            load_planes(1, j, 1)
         w_raw = keep.tile([P, PACK, M], F32, name="w_raw")
         nc.sync.dma_start(out=w_raw[:], in_=w.rearrange("(p j) m -> p j m", j=PACK))
 
@@ -76,8 +75,15 @@ def tile_attend_aq_kernel(tc, cb, w, norm, offs, out):
         e_codes = keep.tile([P, COLS], U32, name="e_codes", align_bytes=64)
         e_scales = keep.tile([P, COLS], U8, name="e_scales", align_bytes=64)
         picked = [keep.tile([P, COLS], F32, name=f"picked{j}") for j in range(PACK)]
-        summed = [keep.tile([P, COLS], F32, name=f"summed{j}") for j in range(PACK)]
+        summed = [keep.tile([P, COLS], F32, name=f"summed{j}") for j in range(LAST)]
         rounded = [keep.tile([P, COLS], BF16, name=f"rounded{j}") for j in range(PACK)]
+
+        ring = [keep.tile([P, P], F32, name=f"ring{r}") for r in range(3)]
+
+        def sum_of(j, lo, hi):
+            if j < LAST:
+                return summed[j][:, lo:hi]
+            return ring[CHUNKS.index((lo, hi)) % 3][:, 0 : hi - lo]
 
         def entries(o, lo, hi):
             first = o * COLS // 16
@@ -88,7 +94,7 @@ def tile_attend_aq_kernel(tc, cb, w, norm, offs, out):
 
         def gather(o, j, lo, hi):
             nc.vector.tensor_tensor(
-                summed[j][:, lo:hi], whole[o, j].indirect(entries(o, lo, hi)), picked[j][:, lo:hi], ADD
+                sum_of(j, lo, hi), whole[o, j].indirect(entries(o, lo, hi)), picked[j][:, lo:hi], ADD
             )
 
         def add(j, lo, hi):
@@ -96,7 +102,7 @@ def tile_attend_aq_kernel(tc, cb, w, norm, offs, out):
                 target = e_last[:, lo - SPLIT : hi - SPLIT, j]
             else:
                 target = rounded[j][:, lo:hi]
-            nc.vector.tensor_tensor(target, summed[j][:, lo:hi], norm_all[:, lo:hi], MULT)
+            nc.vector.tensor_tensor(target, sum_of(j, lo, hi), norm_all[:, lo:hi], MULT)
 
         def interleave(j, lo, hi):
             if lo >= SPLIT:
@@ -104,27 +110,26 @@ def tile_attend_aq_kernel(tc, cb, w, norm, offs, out):
             else:
                 nc.scalar.copy(out=e_main[:, lo:hi, j], in_=rounded[j][:, lo:hi])
 
-        pick(0, 0)
-        pick(0, 1)
-        gather(1, 1, 0, COLS)
-        pick(1, 2)
-        add(1, 0, COLS)
-        interleave(1, 0, SPLIT)
-        interleave(1, SPLIT, COLS)
-        gather(1, 0, 0, COLS)
-        add(0, 0, COLS)
-        interleave(0, 0, SPLIT)
-        interleave(0, SPLIT, COLS)
-        gather(0, 2, 0, COLS)
-        add(2, 0, SPLIT)
-        interleave(2, 0, SPLIT)
-        add(2, SPLIT, COLS)
-        pick(1, LAST)
+        for j in range(LAST):
+            pick(0, j)
+            gather(1, j, 0, COLS)
+            if j < 2:
+                add(j, 0, COLS)
+                interleave(j, 0, SPLIT)
+                interleave(j, SPLIT, COLS)
+            else:
+                add(j, 0, SPLIT)
+                interleave(j, 0, SPLIT)
+                add(j, SPLIT, COLS)
+        pick(0, LAST)
 
         w_grouped = keep.tile([P, M, PACK], BF16, name="w_grouped", align_bytes=64)
         w_codes = keep.tile([P, M], U32, name="w_codes", align_bytes=64)
         w_scales = keep.tile([P, M], U8, name="w_scales", align_bytes=64)
-        nc.scalar.copy(out=w_grouped[:], in_=w_raw[:].rearrange("p j m -> p m j"))
+        nc.scalar.copy(
+            out=w_grouped[:].rearrange("p (c i) j -> p c j i", i=4),
+            in_=w_raw[:].rearrange("p j (c i) -> p c j i", i=4),
+        )
 
         def quantise(lo, hi):
             if lo >= SPLIT:
@@ -138,7 +143,7 @@ def tile_attend_aq_kernel(tc, cb, w, norm, offs, out):
             )
 
         banks = {}
-        for name, lo, hi in (("y0", 0, 256), ("y1", 256, 448), ("y2", 448, 512)):
+        for name, lo, hi in (("y0", 0, 256), ("y1", 256, 384), ("y2", 384, 448), ("y3", 448, 512)):
             banks[lo, hi] = psum.tile([P, hi - lo], F32, name=name)
         result = keep.tile([P, COLS], F32, name="result")
 
@@ -155,40 +160,46 @@ def tile_attend_aq_kernel(tc, cb, w, norm, offs, out):
                         stop=True,
                     )
 
-        def finish(lo, hi):
-            if hi == COLS:
+        def evacuate(lo, hi):
+            if lo >= 384:
                 nc.vector.tensor_copy(out=result[:, lo:hi], in_=banks[lo, hi][:])
             else:
                 nc.scalar.copy(out=result[:, lo:hi], in_=banks[lo, hi][:])
-            nc.sync.dma_start(out=out[:, lo:hi], in_=result[:, lo:hi])
 
-        gather(0, LAST, *CHUNKS[0])
-        gather(0, LAST, *CHUNKS[1])
+        def store(queue, lo, hi):
+            queue.dma_start(out=out[:, lo:hi], in_=result[:, lo:hi])
+
+        gather(1, LAST, *CHUNKS[0])
+        gather(1, LAST, *CHUNKS[1])
         add(LAST, *CHUNKS[0])
         interleave(LAST, *CHUNKS[0])
-        gather(0, LAST, *CHUNKS[2])
+        gather(1, LAST, *CHUNKS[2])
         add(LAST, *CHUNKS[1])
         interleave(LAST, *CHUNKS[1])
-        gather(0, LAST, *CHUNKS[3])
+        gather(1, LAST, *CHUNKS[3])
         add(LAST, *CHUNKS[2])
         interleave(LAST, *CHUNKS[2])
+        gather(1, LAST, *CHUNKS[4])
+        add(LAST, *CHUNKS[3])
+        interleave(LAST, *CHUNKS[3])
         nc.vector.quantize_mx(
             out=w_codes[:].bitcast(FP8X4), scales=w_scales[:], in_=w_grouped[:].rearrange("p m j -> p (m j)")
         )
-        gather(0, LAST, *CHUNKS[4])
-        add(LAST, *CHUNKS[3])
-        interleave(LAST, *CHUNKS[3])
         quantise(*CHUNKS[0])
         multiply(*CHUNKS[0])
         add(LAST, *CHUNKS[4])
         quantise(*CHUNKS[1])
         multiply(*CHUNKS[1])
-        finish(0, 256)
-        quantise(*CHUNKS[2])
-        multiply(*CHUNKS[2])
-        quantise(*CHUNKS[3])
-        multiply(*CHUNKS[3])
-        finish(256, 448)
+        evacuate(0, 256)
+        store(nc.sync, 0, 256)
         quantise(*CHUNKS[4])
         multiply(*CHUNKS[4])
-        finish(448, 512)
+        quantise(*CHUNKS[2])
+        multiply(*CHUNKS[2])
+        evacuate(256, 384)
+        store(nc.scalar, 256, 384)
+        quantise(*CHUNKS[3])
+        multiply(*CHUNKS[3])
+        evacuate(448, 512)
+        evacuate(384, 448)
+        store(nc.sync, 384, 512)

@@ -78,12 +78,12 @@ def tile_attend_aq_kernel(tc, cb, w, norm, offs, out):
         summed = [keep.tile([P, COLS], F32, name=f"summed{j}") for j in range(LAST)]
         rounded = [keep.tile([P, COLS], BF16, name=f"rounded{j}") for j in range(PACK)]
 
-        ring = [keep.tile([P, P], F32, name=f"ring{r}") for r in range(3)]
+        ring = keep.tile([P, 384], F32, name="ring")
 
         def sum_of(j, lo, hi):
             if j < LAST:
                 return summed[j][:, lo:hi]
-            return ring[CHUNKS.index((lo, hi)) % 3][:, 0 : hi - lo]
+            return ring[:, lo % 384 : lo % 384 + hi - lo]
 
         def entries(o, lo, hi):
             first = o * COLS // 16
@@ -143,7 +143,7 @@ def tile_attend_aq_kernel(tc, cb, w, norm, offs, out):
             )
 
         banks = {}
-        for name, lo, hi in (("y0", 0, 256), ("y1", 256, 384), ("y2", 384, 448), ("y3", 448, 512)):
+        for name, lo, hi in (("y0", 0, 128), ("y4", 128, 256), ("y1", 256, 384), ("y2", 384, 448), ("y3", 448, 512)):
             banks[lo, hi] = psum.tile([P, hi - lo], F32, name=name)
         result = keep.tile([P, COLS], F32, name="result")
 
@@ -169,17 +169,15 @@ def tile_attend_aq_kernel(tc, cb, w, norm, offs, out):
         def store(queue, lo, hi):
             queue.dma_start(out=out[:, lo:hi], in_=result[:, lo:hi])
 
-        gather(1, LAST, *CHUNKS[0])
-        gather(1, LAST, *CHUNKS[1])
+        gather(1, LAST, 0, 256)
         add(LAST, *CHUNKS[0])
         interleave(LAST, *CHUNKS[0])
         gather(1, LAST, *CHUNKS[2])
         add(LAST, *CHUNKS[1])
         interleave(LAST, *CHUNKS[1])
-        gather(1, LAST, *CHUNKS[3])
+        gather(1, LAST, 384, COLS)
         add(LAST, *CHUNKS[2])
         interleave(LAST, *CHUNKS[2])
-        gather(1, LAST, *CHUNKS[4])
         add(LAST, *CHUNKS[3])
         interleave(LAST, *CHUNKS[3])
         nc.vector.quantize_mx(
@@ -187,17 +185,19 @@ def tile_attend_aq_kernel(tc, cb, w, norm, offs, out):
         )
         quantise(*CHUNKS[0])
         multiply(*CHUNKS[0])
+        evacuate(0, 128)
+        store(nc.sync, 0, 128)
         add(LAST, *CHUNKS[4])
         quantise(*CHUNKS[1])
         multiply(*CHUNKS[1])
-        evacuate(0, 256)
-        store(nc.sync, 0, 256)
-        quantise(*CHUNKS[4])
-        multiply(*CHUNKS[4])
+        evacuate(128, 256)
+        store(nc.sync, 128, 256)
         quantise(*CHUNKS[2])
         multiply(*CHUNKS[2])
         evacuate(256, 384)
         store(nc.scalar, 256, 384)
+        quantise(*CHUNKS[4])
+        multiply(*CHUNKS[4])
         quantise(*CHUNKS[3])
         multiply(*CHUNKS[3])
         evacuate(448, 512)

@@ -186,20 +186,18 @@ def tile_attend_aq_kernel(tc, cb, w, norm, offs, out):
         quantise(*CHUNKS[0])
         multiply(*CHUNKS[0])
         evacuate(0, 128)
-        store(nc.sync, 0, 128)
         add(LAST, *CHUNKS[4])
         quantise(*CHUNKS[1])
         multiply(*CHUNKS[1])
         evacuate(128, 256)
-        store(nc.sync, 128, 256)
+        store(nc.sync, 0, 256)
         quantise(*CHUNKS[2])
         multiply(*CHUNKS[2])
         evacuate(256, 384)
-        store(nc.scalar, 256, 384)
         quantise(*CHUNKS[4])
         multiply(*CHUNKS[4])
         quantise(*CHUNKS[3])
         multiply(*CHUNKS[3])
         evacuate(448, 512)
         evacuate(384, 448)
-        store(nc.sync, 384, 512)
+        store(nc.sync, 256, 512)

@@ -70,10 +70,14 @@ def tile_attend_aq_kernel(tc, cb, w, norm, offs, out):
         norm_all = keep.tile([P, COLS], F32, name="norm_all")
         nc.scalar.copy(out=norm_all[:], in_=norm_spread[:])
 
-        e_main = keep.tile([P, SPLIT, PACK], BF16, name="e_main", align_bytes=64)
+        grouped = keep.tile([P, M + SPLIT, PACK], BF16, name="grouped", align_bytes=64)
+        w_grouped = grouped[:, 0:M, :]
+        e_main = grouped[:, M:, :]
         e_last = keep.tile([P, COLS - SPLIT, PACK], BF16, name="e_last", align_bytes=64)
-        e_codes = keep.tile([P, COLS], U32, name="e_codes", align_bytes=64)
-        e_scales = keep.tile([P, COLS], U8, name="e_scales", align_bytes=64)
+        codes = keep.tile([P, M + COLS], U32, name="codes", align_bytes=64)
+        scales = keep.tile([P, M + COLS], U8, name="scales", align_bytes=64)
+        w_codes, e_codes = codes[:, 0:M], codes[:, M:]
+        w_scales, e_scales = scales[:, 0:M], scales[:, M:]
         picked = [keep.tile([P, COLS], F32, name=f"picked{j}") for j in range(PACK)]
         summed = [keep.tile([P, COLS], F32, name=f"summed{j}") for j in range(LAST)]
         rounded = [keep.tile([P, COLS], BF16, name=f"rounded{j}") for j in range(PACK)]
@@ -123,11 +127,8 @@ def tile_attend_aq_kernel(tc, cb, w, norm, offs, out):
                 add(j, SPLIT, COLS)
         pick(0, LAST)
 
-        w_grouped = keep.tile([P, M, PACK], BF16, name="w_grouped", align_bytes=64)
-        w_codes = keep.tile([P, M], U32, name="w_codes", align_bytes=64)
-        w_scales = keep.tile([P, M], U8, name="w_scales", align_bytes=64)
         nc.scalar.copy(
-            out=w_grouped[:].rearrange("p (c i) j -> p c j i", i=4),
+            out=w_grouped.rearrange("p (c i) j -> p c j i", i=4),
             in_=w_raw[:].rearrange("p j (c i) -> p c j i", i=4),
         )
 
@@ -152,8 +153,8 @@ def tile_attend_aq_kernel(tc, cb, w, norm, offs, out):
                 if blo <= lo and hi <= bhi:
                     nc.tensor.matmul_mx(
                         out=bank[:, lo - blo : hi - blo],
-                        lhsT=w_codes[:].bitcast(FP8X4),
-                        lhsT_scale=w_scales[:],
+                        lhsT=w_codes.bitcast(FP8X4),
+                        lhsT_scale=w_scales,
                         rhs=e_codes[:, lo:hi].bitcast(FP8X4),
                         rhs_scale=e_scales[:, lo:hi],
                         start=True,
@@ -181,9 +182,10 @@ def tile_attend_aq_kernel(tc, cb, w, norm, offs, out):
         add(LAST, *CHUNKS[3])
         interleave(LAST, *CHUNKS[3])
         nc.vector.quantize_mx(
-            out=w_codes[:].bitcast(FP8X4), scales=w_scales[:], in_=w_grouped[:].rearrange("p m j -> p (m j)")
+            out=codes[:, 0 : M + P].bitcast(FP8X4),
+            scales=scales[:, 0 : M + P],
+            in_=grouped[:, 0 : M + P, :].rearrange("p n j -> p (n j)"),
         )
-        quantise(*CHUNKS[0])
         multiply(*CHUNKS[0])
         evacuate(0, 128)
         add(LAST, *CHUNKS[4])
@@ -191,11 +193,11 @@ def tile_attend_aq_kernel(tc, cb, w, norm, offs, out):
         multiply(*CHUNKS[1])
         evacuate(128, 256)
         store(nc.sync, 0, 256)
+        quantise(*CHUNKS[4])
+        multiply(*CHUNKS[4])
         quantise(*CHUNKS[2])
         multiply(*CHUNKS[2])
         evacuate(256, 384)
-        quantise(*CHUNKS[4])
-        multiply(*CHUNKS[4])
         quantise(*CHUNKS[3])
         multiply(*CHUNKS[3])
         evacuate(448, 512)

@@ -21,7 +21,6 @@ M = 128
 FLOPS = 2 * 512 * COLS * M
 
 CHUNKS = ((0, 128), (128, 256), (256, 384), (384, 448), (448, 512))
-SPLIT = 448
 LAST = PACK - 1
 
 
@@ -70,17 +69,20 @@ def tile_attend_aq_kernel(tc, cb, w, norm, offs, out):
         norm_all = keep.tile([P, COLS], F32, name="norm_all")
         nc.scalar.copy(out=norm_all[:], in_=norm_spread[:])
 
-        grouped = keep.tile([P, M + SPLIT, PACK], BF16, name="grouped", align_bytes=64)
-        w_grouped = grouped[:, 0:M, :]
-        e_main = grouped[:, M:, :]
-        e_last = keep.tile([P, COLS - SPLIT, PACK], BF16, name="e_last", align_bytes=64)
+        grouped = {}
+        pairs = {}
+        for lo, hi in CHUNKS:
+            lead = M if lo == 0 else 0
+            grouped[lo] = keep.tile([P, lead + hi - lo, PACK], BF16, name=f"grouped{lo}", align_bytes=64)
+            pairs[lo] = keep.tile([P, 2, hi - lo, 2], BF16, name=f"pairs{lo}", align_bytes=64)
+        w_grouped = grouped[0][:, 0:M, :]
         codes = keep.tile([P, M + COLS], U32, name="codes", align_bytes=64)
         scales = keep.tile([P, M + COLS], U8, name="scales", align_bytes=64)
         w_codes, e_codes = codes[:, 0:M], codes[:, M:]
         w_scales, e_scales = scales[:, 0:M], scales[:, M:]
         picked = [keep.tile([P, COLS], F32, name=f"picked{j}") for j in range(PACK)]
         summed = [keep.tile([P, COLS], F32, name=f"summed{j}") for j in range(LAST)]
-        rounded = [keep.tile([P, COLS], BF16, name=f"rounded{j}") for j in range(PACK)]
+        rounded = [keep.tile([P, COLS], BF16, name=f"rounded{j}") for j in range(2)]
 
         ring = keep.tile([P, 384], F32, name="ring")
 
@@ -102,29 +104,24 @@ def tile_attend_aq_kernel(tc, cb, w, norm, offs, out):
             )
 
         def add(j, lo, hi):
-            if lo >= SPLIT and j >= 2:
-                target = e_last[:, lo - SPLIT : hi - SPLIT, j]
-            else:
-                target = rounded[j][:, lo:hi]
-            nc.vector.tensor_tensor(target, sum_of(j, lo, hi), norm_all[:, lo:hi], MULT)
+            nc.vector.tensor_tensor(pairs[lo][:, j // 2, :, j % 2], sum_of(j, lo, hi), norm_all[:, lo:hi], MULT)
 
-        def interleave(j, lo, hi):
-            if lo >= SPLIT:
-                nc.scalar.copy(out=e_last[:, lo - SPLIT : hi - SPLIT, j], in_=rounded[j][:, lo:hi])
-            else:
-                nc.scalar.copy(out=e_main[:, lo:hi, j], in_=rounded[j][:, lo:hi])
+        def interleave(lo, hi):
+            lead = M if lo == 0 else 0
+            words = grouped[lo][:, lead:, :].rearrange("p n j -> p (n j)").bitcast(U32)
+            source = pairs[lo][:].rearrange("p u n e -> p u (n e)").bitcast(U32)
+            nc.scalar.copy(out=words.rearrange("p (n u) -> p n u", u=2), in_=source.rearrange("p u n -> p n u"))
 
         for j in range(LAST):
             pick(0, j)
             gather(1, j, 0, COLS)
             if j < 2:
-                add(j, 0, COLS)
-                interleave(j, 0, SPLIT)
-                interleave(j, SPLIT, COLS)
+                nc.vector.tensor_tensor(rounded[j][:], summed[j][:], norm_all[:], MULT)
+                for lo, hi in CHUNKS:
+                    nc.scalar.copy(out=pairs[lo][:, 0, :, j], in_=rounded[j][:, lo:hi])
             else:
-                add(j, 0, SPLIT)
-                interleave(j, 0, SPLIT)
-                add(j, SPLIT, COLS)
+                for lo, hi in CHUNKS:
+                    add(j, lo, hi)
         pick(0, LAST)
 
         nc.scalar.copy(
@@ -133,10 +130,7 @@ def tile_attend_aq_kernel(tc, cb, w, norm, offs, out):
         )
 
         def quantise(lo, hi):
-            if lo >= SPLIT:
-                source = e_last[:, lo - SPLIT : hi - SPLIT, :]
-            else:
-                source = e_main[:, lo:hi, :]
+            source = grouped[lo][:]
             nc.vector.quantize_mx(
                 out=e_codes[:, lo:hi].bitcast(FP8X4),
                 scales=e_scales[:, lo:hi],
@@ -162,7 +156,7 @@ def tile_attend_aq_kernel(tc, cb, w, norm, offs, out):
                     )
 
         def evacuate(lo, hi):
-            if lo >= 384:
+            if lo >= 448:
                 nc.vector.tensor_copy(out=result[:, lo:hi], in_=banks[lo, hi][:])
             else:
                 nc.scalar.copy(out=result[:, lo:hi], in_=banks[lo, hi][:])
@@ -172,34 +166,35 @@ def tile_attend_aq_kernel(tc, cb, w, norm, offs, out):
 
         gather(1, LAST, 0, 256)
         add(LAST, *CHUNKS[0])
-        interleave(LAST, *CHUNKS[0])
+        interleave(*CHUNKS[0])
         gather(1, LAST, *CHUNKS[2])
         add(LAST, *CHUNKS[1])
-        interleave(LAST, *CHUNKS[1])
+        interleave(*CHUNKS[1])
         gather(1, LAST, 384, COLS)
         add(LAST, *CHUNKS[2])
-        interleave(LAST, *CHUNKS[2])
+        interleave(*CHUNKS[2])
         add(LAST, *CHUNKS[3])
-        interleave(LAST, *CHUNKS[3])
+        interleave(*CHUNKS[3])
+        add(LAST, *CHUNKS[4])
+        interleave(*CHUNKS[4])
         nc.vector.quantize_mx(
             out=codes[:, 0 : M + P].bitcast(FP8X4),
             scales=scales[:, 0 : M + P],
-            in_=grouped[:, 0 : M + P, :].rearrange("p n j -> p (n j)"),
+            in_=grouped[0][:].rearrange("p n j -> p (n j)"),
         )
         multiply(*CHUNKS[0])
         evacuate(0, 128)
-        add(LAST, *CHUNKS[4])
         quantise(*CHUNKS[1])
         multiply(*CHUNKS[1])
         evacuate(128, 256)
         store(nc.sync, 0, 256)
-        quantise(*CHUNKS[4])
-        multiply(*CHUNKS[4])
         quantise(*CHUNKS[2])
         multiply(*CHUNKS[2])
         evacuate(256, 384)
         quantise(*CHUNKS[3])
         multiply(*CHUNKS[3])
-        evacuate(448, 512)
+        quantise(*CHUNKS[4])
+        multiply(*CHUNKS[4])
         evacuate(384, 448)
+        evacuate(448, 512)
         store(nc.sync, 256, 512)

@@ -22,6 +22,8 @@ FLOPS = 2 * 512 * COLS * M
 
 CHUNKS = ((0, 128), (128, 256), (256, 384), (384, 448), (448, 512))
 LAST = PACK - 1
+PLAIN = 128
+IN_PLACE = 448
 
 
 def tile_attend_aq_kernel(tc, cb, w, norm, offs, out):
@@ -66,15 +68,17 @@ def tile_attend_aq_kernel(tc, cb, w, norm, offs, out):
             nc.tensor.transpose(
                 norm_spread[:, b * P : (b + 1) * P], norm_cols[:, b : b + 1].to_broadcast([P, P]), ident[:]
             )
-        norm_all = keep.tile([P, COLS], F32, name="norm_all")
-        nc.scalar.copy(out=norm_all[:], in_=norm_spread[:])
+        norm_all = norm_spread
 
         grouped = {}
         pairs = {}
-        for lo, hi in CHUNKS:
+        for lo in range(0, COLS, P):
             lead = M if lo == 0 else 0
-            grouped[lo] = keep.tile([P, lead + hi - lo, PACK], BF16, name=f"grouped{lo}", align_bytes=64)
-            pairs[lo] = keep.tile([P, 2, hi - lo, 2], BF16, name=f"pairs{lo}", align_bytes=64)
+            grouped[lo] = keep.tile([P, lead + P, PACK], BF16, name=f"grouped{lo}", align_bytes=64)
+        in_place = grouped[384][:, IN_PLACE - 384 :, :]
+        for lo, hi in CHUNKS:
+            if PLAIN <= lo < IN_PLACE:
+                pairs[lo] = keep.tile([P, 2, hi - lo, 2], BF16, name=f"pairs{lo}", align_bytes=64)
         w_grouped = grouped[0][:, 0:M, :]
         codes = keep.tile([P, M + COLS], U32, name="codes", align_bytes=64)
         scales = keep.tile([P, M + COLS], U8, name="scales", align_bytes=64)
@@ -82,14 +86,16 @@ def tile_attend_aq_kernel(tc, cb, w, norm, offs, out):
         w_scales, e_scales = scales[:, 0:M], scales[:, M:]
         picked = [keep.tile([P, COLS], F32, name=f"picked{j}") for j in range(PACK)]
         summed = [keep.tile([P, COLS], F32, name=f"summed{j}") for j in range(LAST)]
-        rounded = [keep.tile([P, COLS], BF16, name=f"rounded{j}") for j in range(2)]
+        rounded = [keep.tile([P, COLS], BF16, name=f"rounded{j}") for j in range(PACK)]
 
-        ring = keep.tile([P, 384], F32, name="ring")
+        tail_sums = keep.tile([P, 384], F32, name="tail_sums")
 
         def sum_of(j, lo, hi):
             if j < LAST:
                 return summed[j][:, lo:hi]
-            return ring[:, lo % 384 : lo % 384 + hi - lo]
+            if lo < 384:
+                return tail_sums[:, lo:hi]
+            return picked[LAST][:, lo - P : hi - P]
 
         def entries(o, lo, hi):
             first = o * COLS // 16
@@ -104,11 +110,23 @@ def tile_attend_aq_kernel(tc, cb, w, norm, offs, out):
             )
 
         def add(j, lo, hi):
-            nc.vector.tensor_tensor(pairs[lo][:, j // 2, :, j % 2], sum_of(j, lo, hi), norm_all[:, lo:hi], MULT)
+            if lo >= IN_PLACE:
+                target = in_place[:, :, j]
+            elif lo < PLAIN:
+                target = rounded[j][:, lo:hi]
+            else:
+                target = pairs[lo][:, j // 2, :, j % 2]
+            nc.vector.tensor_tensor(target, sum_of(j, lo, hi), norm_all[:, lo:hi], MULT)
+
+        def place(j, lo, hi):
+            lead = M if lo == 0 else 0
+            nc.scalar.copy(out=grouped[lo][:, lead:, j], in_=rounded[j][:, lo:hi])
 
         def interleave(lo, hi):
-            lead = M if lo == 0 else 0
-            words = grouped[lo][:, lead:, :].rearrange("p n j -> p (n j)").bitcast(U32)
+            if lo < PLAIN:
+                place(LAST, lo, hi)
+                return
+            words = grouped[lo][:, 0 : hi - lo, :].rearrange("p n j -> p (n j)").bitcast(U32)
             source = pairs[lo][:].rearrange("p u n e -> p u (n e)").bitcast(U32)
             nc.scalar.copy(out=words.rearrange("p (n u) -> p n u", u=2), in_=source.rearrange("p u n -> p n u"))
 
@@ -117,11 +135,17 @@ def tile_attend_aq_kernel(tc, cb, w, norm, offs, out):
             gather(1, j, 0, COLS)
             if j < 2:
                 nc.vector.tensor_tensor(rounded[j][:], summed[j][:], norm_all[:], MULT)
-                for lo, hi in CHUNKS:
-                    nc.scalar.copy(out=pairs[lo][:, 0, :, j], in_=rounded[j][:, lo:hi])
-            else:
-                for lo, hi in CHUNKS:
+            for lo, hi in CHUNKS:
+                if j == 2:
                     add(j, lo, hi)
+                if lo < PLAIN:
+                    place(j, lo, hi)
+                elif j == 2:
+                    continue
+                elif lo >= IN_PLACE:
+                    nc.scalar.copy(out=in_place[:, :, j], in_=rounded[j][:, lo:hi])
+                else:
+                    nc.scalar.copy(out=pairs[lo][:, 0, :, j], in_=rounded[j][:, lo:hi])
         pick(0, LAST)
 
         nc.scalar.copy(
@@ -156,7 +180,7 @@ def tile_attend_aq_kernel(tc, cb, w, norm, offs, out):
                     )
 
         def evacuate(lo, hi):
-            if lo >= 448:
+            if lo == 448:
                 nc.vector.tensor_copy(out=result[:, lo:hi], in_=banks[lo, hi][:])
             else:
                 nc.scalar.copy(out=result[:, lo:hi], in_=banks[lo, hi][:])
@@ -165,9 +189,9 @@ def tile_attend_aq_kernel(tc, cb, w, norm, offs, out):
             queue.dma_start(out=out[:, lo:hi], in_=result[:, lo:hi])
 
         gather(1, LAST, 0, 256)
+        gather(1, LAST, *CHUNKS[2])
         add(LAST, *CHUNKS[0])
         interleave(*CHUNKS[0])
-        gather(1, LAST, *CHUNKS[2])
         add(LAST, *CHUNKS[1])
         interleave(*CHUNKS[1])
         gather(1, LAST, 384, COLS)
@@ -176,7 +200,6 @@ def tile_attend_aq_kernel(tc, cb, w, norm, offs, out):
         add(LAST, *CHUNKS[3])
         interleave(*CHUNKS[3])
         add(LAST, *CHUNKS[4])
-        interleave(*CHUNKS[4])
         nc.vector.quantize_mx(
             out=codes[:, 0 : M + P].bitcast(FP8X4),
             scales=scales[:, 0 : M + P],
@@ -191,9 +214,8 @@ def tile_attend_aq_kernel(tc, cb, w, norm, offs, out):
         quantise(*CHUNKS[2])
         multiply(*CHUNKS[2])
         evacuate(256, 384)
-        quantise(*CHUNKS[3])
+        quantise(384, COLS)
         multiply(*CHUNKS[3])
-        quantise(*CHUNKS[4])
         multiply(*CHUNKS[4])
         evacuate(384, 448)
         evacuate(448, 512)

@@ -11,6 +11,7 @@ U8 = mybir.dt.uint8
 FP8X4 = mybir.dt.float8_e4m3fn_x4
 MULT = mybir.AluOpType.mult
 ADD = mybir.AluOpType.add
+COPY = mybir.ActivationFunctionType.Copy
 
 P = 128
 PACK = 4
@@ -22,7 +23,8 @@ FLOPS = 2 * 512 * COLS * M
 
 CHUNKS = ((0, 128), (128, 256), (256, 384), (384, 448), (448, 512))
 LAST = PACK - 1
-PLAIN = 128
+PLAIN = 0
+SHARED = 256
 IN_PLACE = 448
 
 
@@ -88,14 +90,13 @@ def tile_attend_aq_kernel(tc, cb, w, norm, offs, out):
         summed = [keep.tile([P, COLS], F32, name=f"summed{j}") for j in range(LAST)]
         rounded = [keep.tile([P, COLS], BF16, name=f"rounded{j}") for j in range(PACK)]
 
-        tail_sums = keep.tile([P, 384], F32, name="tail_sums")
+        tail_sums = keep.tile([P, COLS], F32, name="tail_sums")
+        tail_picked = keep.tile([P, COLS - SHARED], F32, name="tail_picked")
 
         def sum_of(j, lo, hi):
             if j < LAST:
                 return summed[j][:, lo:hi]
-            if lo < 384:
-                return tail_sums[:, lo:hi]
-            return picked[LAST][:, lo - P : hi - P]
+            return tail_sums[:, lo:hi]
 
         def entries(o, lo, hi):
             first = o * COLS // 16
@@ -126,7 +127,8 @@ def tile_attend_aq_kernel(tc, cb, w, norm, offs, out):
             if lo < PLAIN:
                 place(LAST, lo, hi)
                 return
-            words = grouped[lo][:, 0 : hi - lo, :].rearrange("p n j -> p (n j)").bitcast(U32)
+            lead = M if lo == 0 else 0
+            words = grouped[lo][:, lead : lead + hi - lo, :].rearrange("p n j -> p (n j)").bitcast(U32)
             source = pairs[lo][:].rearrange("p u n e -> p u (n e)").bitcast(U32)
             nc.scalar.copy(out=words.rearrange("p (n u) -> p n u", u=2), in_=source.rearrange("p u n -> p n u"))
 
@@ -147,6 +149,7 @@ def tile_attend_aq_kernel(tc, cb, w, norm, offs, out):
                 else:
                     nc.scalar.copy(out=pairs[lo][:, 0, :, j], in_=rounded[j][:, lo:hi])
         pick(0, LAST)
+        nc.scalar.activation(tail_picked[:], whole[1, LAST].indirect(entries(1, SHARED, COLS)), COPY)
 
         nc.scalar.copy(
             out=w_grouped.rearrange("p (c i) j -> p c j i", i=4),
@@ -188,13 +191,16 @@ def tile_attend_aq_kernel(tc, cb, w, norm, offs, out):
         def store(queue, lo, hi):
             queue.dma_start(out=out[:, lo:hi], in_=result[:, lo:hi])
 
-        gather(1, LAST, 0, 256)
-        gather(1, LAST, *CHUNKS[2])
+        gather(1, LAST, *CHUNKS[0])
+        gather(1, LAST, *CHUNKS[1])
         add(LAST, *CHUNKS[0])
         interleave(*CHUNKS[0])
         add(LAST, *CHUNKS[1])
         interleave(*CHUNKS[1])
-        gather(1, LAST, 384, COLS)
+        for lo in range(SHARED, COLS, P):
+            nc.vector.tensor_tensor(
+                tail_sums[:, lo : lo + P], tail_picked[:, lo - SHARED : lo - SHARED + P], picked[LAST][:, lo : lo + P], ADD
+            )
         add(LAST, *CHUNKS[2])
         interleave(*CHUNKS[2])
         add(LAST, *CHUNKS[3])

@@ -61,8 +61,8 @@ def tile_attend_aq_kernel(tc, cb, w, norm, offs, out):
 
         ident = keep.tile([P, P], F32, name="ident")
         make_identity(nc, ident[:])
-        norm_turned = psum.tile([P, P], F32, name="norm_turned")
-        nc.tensor.transpose(norm_turned[:], norm_rows[:], ident[:])
+        norm_turned = psum.tile([P, COLS], F32, name="norm_turned", tag="turned")
+        nc.tensor.transpose(norm_turned[:, 0:P], norm_rows[:], ident[:])
         norm_cols = keep.tile([P, 4], F32, name="norm_cols")
         nc.scalar.copy(out=norm_cols[:], in_=norm_turned[:, 0:4])
         norm_spread = psum.tile([P, COLS], F32, name="norm_spread")
@@ -148,13 +148,27 @@ def tile_attend_aq_kernel(tc, cb, w, norm, offs, out):
                     nc.scalar.copy(out=in_place[:, :, j], in_=rounded[j][:, lo:hi])
                 else:
                     nc.scalar.copy(out=pairs[lo][:, 0, :, j], in_=rounded[j][:, lo:hi])
-        pick(0, LAST)
-        nc.scalar.activation(tail_picked[:], whole[1, LAST].indirect(entries(1, SHARED, COLS)), COPY)
+        nc.scalar.activation(picked[LAST][:, SHARED:], whole[0, LAST].indirect(entries(0, SHARED, COLS)), COPY)
+        nc.vector.tensor_copy(picked[LAST][:, 0:SHARED], whole[0, LAST].indirect(entries(0, 0, SHARED)))
+        turned = psum.tile([P, COLS], F32, name="turned", tag="turned")
+        staged = keep.tile([P, COLS], F32, name="staged")
+        banked = psum.tile([P, COLS], F32, name="banked")
+        for lo in range(SHARED, COLS, P):
+            nc.tensor.transpose(turned[:, lo : lo + P], picked[LAST][:, lo : lo + P], ident[:])
+        nc.scalar.copy(out=staged[:, SHARED:], in_=turned[:, SHARED:])
+        for lo in range(SHARED, COLS, P):
+            nc.tensor.transpose(banked[:, lo : lo + P], staged[:, lo : lo + P], ident[:])
+        for lo in range(SHARED, COLS, P):
+            nc.scalar.activation(
+                tail_picked[:, lo - SHARED : lo - SHARED + P], whole[1, LAST].indirect(entries(1, lo, lo + P)), COPY
+            )
 
-        nc.scalar.copy(
-            out=w_grouped.rearrange("p (c i) j -> p c j i", i=4),
-            in_=w_raw[:].rearrange("p j (c i) -> p c j i", i=4),
-        )
+        nc.gpsimd.tensor_scalar(w_grouped, w_raw[:].rearrange("p j m -> p m j"), 1.0, 0.0, MULT, ADD)
+
+        def plain_add(lo):
+            nc.vector.tensor_tensor(
+                tail_sums[:, lo : lo + P], tail_picked[:, lo - SHARED : lo - SHARED + P], banked[:, lo : lo + P], ADD
+            )
 
         def quantise(lo, hi):
             source = grouped[lo][:]
@@ -197,10 +211,8 @@ def tile_attend_aq_kernel(tc, cb, w, norm, offs, out):
         interleave(*CHUNKS[0])
         add(LAST, *CHUNKS[1])
         interleave(*CHUNKS[1])
-        for lo in range(SHARED, COLS, P):
-            nc.vector.tensor_tensor(
-                tail_sums[:, lo : lo + P], tail_picked[:, lo - SHARED : lo - SHARED + P], picked[LAST][:, lo : lo + P], ADD
-            )
+        plain_add(256)
+        plain_add(384)
         add(LAST, *CHUNKS[2])
         interleave(*CHUNKS[2])
         add(LAST, *CHUNKS[3])

@@ -23,7 +23,7 @@ FLOPS = 2 * 512 * COLS * M
 
 CHUNKS = ((0, 128), (128, 256), (256, 384), (384, 448), (448, 512))
 LAST = PACK - 1
-PLAIN = 0
+PLAIN = 128
 SHARED = 256
 IN_PLACE = 448
 
@@ -48,12 +48,12 @@ def tile_attend_aq_kernel(tc, cb, w, norm, offs, out):
         norm_rows = keep.tile([P, P], F32, name="norm_rows")
         nc.gpsimd.memset(norm_rows[:], 0.0)
 
-        load_planes(0, 0, 1)
+        load_planes(0, 0, 2)
         nc.sync.dma_start(out=norm_rows[0:4, :], in_=norm[0:1, :].rearrange("o (b j) -> (o b) j", b=4))
         offsets = keep.tile([P, BOOKS * COLS // 16], U16, name="offsets")
         nc.sync.dma_start(offsets[:], offs)
-        load_planes(1, 0, 1)
-        for j in range(1, PACK):
+        load_planes(1, 0, 2)
+        for j in range(2, PACK):
             load_planes(0, j, 1)
             load_planes(1, j, 1)
         w_raw = keep.tile([P, PACK, M], F32, name="w_raw")
@@ -88,7 +88,13 @@ def tile_attend_aq_kernel(tc, cb, w, norm, offs, out):
         w_scales, e_scales = scales[:, 0:M], scales[:, M:]
         picked = [keep.tile([P, COLS], F32, name=f"picked{j}") for j in range(PACK)]
         summed = [keep.tile([P, COLS], F32, name=f"summed{j}") for j in range(LAST)]
-        rounded = [keep.tile([P, COLS], BF16, name=f"rounded{j}") for j in range(PACK)]
+        rounded = keep.tile([P, 2, COLS], BF16, name="rounded")
+        last_rounded = keep.tile([P, PLAIN], BF16, name="last_rounded")
+
+        def words_of(lo, hi):
+            first = lo // P * P
+            lead = M if first == 0 else 0
+            return grouped[first][:, lead + lo - first : lead + hi - first, :]
 
         tail_sums = keep.tile([P, COLS], F32, name="tail_sums")
         tail_picked = keep.tile([P, COLS - SHARED], F32, name="tail_picked")
@@ -114,14 +120,13 @@ def tile_attend_aq_kernel(tc, cb, w, norm, offs, out):
             if lo >= IN_PLACE:
                 target = in_place[:, :, j]
             elif lo < PLAIN:
-                target = rounded[j][:, lo:hi]
+                target = last_rounded[:, lo:hi] if j == LAST else words_of(lo, hi)[:, :, j]
             else:
                 target = pairs[lo][:, j // 2, :, j % 2]
             nc.vector.tensor_tensor(target, sum_of(j, lo, hi), norm_all[:, lo:hi], MULT)
 
         def place(j, lo, hi):
-            lead = M if lo == 0 else 0
-            nc.scalar.copy(out=grouped[lo][:, lead:, j], in_=rounded[j][:, lo:hi])
+            nc.scalar.copy(out=words_of(lo, hi)[:, :, j], in_=last_rounded[:, lo:hi])
 
         def interleave(lo, hi):
             if lo < PLAIN:
@@ -132,22 +137,28 @@ def tile_attend_aq_kernel(tc, cb, w, norm, offs, out):
             source = pairs[lo][:].rearrange("p u n e -> p u (n e)").bitcast(U32)
             nc.scalar.copy(out=words.rearrange("p (n u) -> p n u", u=2), in_=source.rearrange("p u n -> p n u"))
 
+        other = keep.tile([P, COLS], F32, name="other")
         for j in range(LAST):
-            pick(0, j)
-            gather(1, j, 0, COLS)
+            if j == 2:
+                nc.scalar.activation(picked[j][:], whole[0, j].indirect(entries(0, 0, COLS)), COPY)
+            else:
+                pick(0, j)
+            if j == 1:
+                nc.vector.tensor_copy(other[:], windows[1, 1].indirect(entries(1, 0, COLS)))
+                nc.vector.tensor_tensor(summed[j][:], other[:], picked[j][:], ADD)
+            else:
+                gather(1, j, 0, COLS)
             if j < 2:
-                nc.vector.tensor_tensor(rounded[j][:], summed[j][:], norm_all[:], MULT)
+                nc.vector.tensor_tensor(rounded[:, j, :], summed[j][:], norm_all[:], MULT)
             for lo, hi in CHUNKS:
                 if j == 2:
                     add(j, lo, hi)
-                if lo < PLAIN:
-                    place(j, lo, hi)
-                elif j == 2:
-                    continue
-                elif lo >= IN_PLACE:
-                    nc.scalar.copy(out=in_place[:, :, j], in_=rounded[j][:, lo:hi])
-                else:
-                    nc.scalar.copy(out=pairs[lo][:, 0, :, j], in_=rounded[j][:, lo:hi])
+                if j == 1:
+                    target = pairs[lo][:, 0, :, :] if lo in pairs else words_of(lo, hi)[:, :, 0:2]
+                    nc.scalar.copy(
+                        out=target.rearrange("p (c i) e -> p c e i", i=4),
+                        in_=rounded[:, :, lo:hi].rearrange("p e (c i) -> p c e i", i=4),
+                    )
         nc.scalar.activation(picked[LAST][:, SHARED:], whole[0, LAST].indirect(entries(0, SHARED, COLS)), COPY)
         nc.vector.tensor_copy(picked[LAST][:, 0:SHARED], whole[0, LAST].indirect(entries(0, 0, SHARED)))
         turned = psum.tile([P, COLS], F32, name="turned", tag="turned")

@@ -159,14 +159,17 @@ def tile_attend_aq_kernel(tc, cb, w, norm, offs, out):
                         out=target.rearrange("p (c i) e -> p c e i", i=4),
                         in_=rounded[:, :, lo:hi].rearrange("p e (c i) -> p c e i", i=4),
                     )
-        nc.scalar.activation(picked[LAST][:, SHARED:], whole[0, LAST].indirect(entries(0, SHARED, COLS)), COPY)
         nc.vector.tensor_copy(picked[LAST][:, 0:SHARED], whole[0, LAST].indirect(entries(0, 0, SHARED)))
-        turned = psum.tile([P, COLS], F32, name="turned", tag="turned")
         staged = keep.tile([P, COLS], F32, name="staged")
         banked = psum.tile([P, COLS], F32, name="banked")
-        for lo in range(SHARED, COLS, P):
-            nc.tensor.transpose(turned[:, lo : lo + P], picked[LAST][:, lo : lo + P], ident[:])
-        nc.scalar.copy(out=staged[:, SHARED:], in_=turned[:, SHARED:])
+        turned = {}
+        for lo, tag in ((256, "turned"), (384, "y3")):
+            hi = lo + P
+            nc.scalar.activation(picked[LAST][:, lo:hi], whole[0, LAST].indirect(entries(0, lo, hi)), COPY)
+            turned[lo] = psum.tile([P, P], F32, name=f"turned{lo}", tag=tag)
+            nc.tensor.transpose(turned[lo][:], picked[LAST][:, lo:hi], ident[:])
+        nc.scalar.copy(out=staged[:, 256:384], in_=turned[256][:])
+        nc.vector.tensor_copy(out=staged[:, 384:512], in_=turned[384][:])
         for lo in range(SHARED, COLS, P):
             nc.tensor.transpose(banked[:, lo : lo + P], staged[:, lo : lo + P], ident[:])
         for lo in range(SHARED, COLS, P):
@@ -191,7 +194,7 @@ def tile_attend_aq_kernel(tc, cb, w, norm, offs, out):
 
         banks = {}
         for name, lo, hi in (("y0", 0, 128), ("y4", 128, 256), ("y1", 256, 384), ("y2", 384, 448), ("y3", 448, 512)):
-            banks[lo, hi] = psum.tile([P, hi - lo], F32, name=name)
+            banks[lo, hi] = psum.tile([P, hi - lo], F32, name=name, tag=name)
         result = keep.tile([P, COLS], F32, name="result")
 
         def multiply(lo, hi):

@@ -21,11 +21,11 @@ COLS = 512
 M = 128
 FLOPS = 2 * 512 * COLS * M
 
+HALF = COLS // 2
 CHUNKS = ((0, 128), (128, 256), (256, 384), (384, 448), (448, 512))
-LAST = PACK - 1
-PLAIN = 128
-SHARED = 256
+PLAIN = 0
 IN_PLACE = 448
+TURNED = 384
 
 
 def tile_attend_aq_kernel(tc, cb, w, norm, offs, out):
@@ -35,220 +35,228 @@ def tile_attend_aq_kernel(tc, cb, w, norm, offs, out):
         psum = ctx.enter_context(tc.psum_pool(name="psum", bufs=1))
 
         rows = cb.rearrange("o (p j) c -> o p (j c)", j=PACK)
-        windows = {}
-        whole = {}
 
         def load_planes(o, first, count):
             tile = keep.tile([P, count * CODEWORDS], F32, name=f"planes{o}{first}")
             nc.sync.dma_start(out=tile[:], in_=rows[o, :, first * CODEWORDS : (first + count) * CODEWORDS])
-            whole[o, first] = tile[:]
-            for j in range(count):
-                windows[o, first + j] = tile[:, j * CODEWORDS : (j + 1) * CODEWORDS]
+            return tile
 
         norm_rows = keep.tile([P, P], F32, name="norm_rows")
         nc.gpsimd.memset(norm_rows[:], 0.0)
 
-        load_planes(0, 0, 2)
-        nc.sync.dma_start(out=norm_rows[0:4, :], in_=norm[0:1, :].rearrange("o (b j) -> (o b) j", b=4))
+        book0 = load_planes(0, 0, 4)
         offsets = keep.tile([P, BOOKS * COLS // 16], U16, name="offsets")
+        nc.sync.dma_start(out=norm_rows[0:4, :], in_=norm[0:1, :].rearrange("o (b j) -> (o b) j", b=4))
         nc.sync.dma_start(offsets[:], offs)
-        load_planes(1, 0, 2)
-        for j in range(2, PACK):
-            load_planes(0, j, 1)
-            load_planes(1, j, 1)
+        book1_01 = load_planes(1, 0, 2)
+        book1_2 = load_planes(1, 2, 1)
+        book1_3 = load_planes(1, 3, 1)
         w_raw = keep.tile([P, PACK, M], F32, name="w_raw")
         nc.sync.dma_start(out=w_raw[:], in_=w.rearrange("(p j) m -> p j m", j=PACK))
 
         ident = keep.tile([P, P], F32, name="ident")
         make_identity(nc, ident[:])
-        norm_turned = psum.tile([P, COLS], F32, name="norm_turned", tag="turned")
-        nc.tensor.transpose(norm_turned[:, 0:P], norm_rows[:], ident[:])
+        norm_turned = psum.tile([P, P], F32, name="norm_turned", tag="spare")
+        nc.tensor.transpose(norm_turned[:], norm_rows[:], ident[:])
         norm_cols = keep.tile([P, 4], F32, name="norm_cols")
         nc.scalar.copy(out=norm_cols[:], in_=norm_turned[:, 0:4])
-        norm_spread = psum.tile([P, COLS], F32, name="norm_spread")
+        norm_all = psum.tile([P, COLS], F32, name="norm_all")
         for b in range(4):
             nc.tensor.transpose(
-                norm_spread[:, b * P : (b + 1) * P], norm_cols[:, b : b + 1].to_broadcast([P, P]), ident[:]
+                norm_all[:, b * P : (b + 1) * P], norm_cols[:, b : b + 1].to_broadcast([P, P]), ident[:]
             )
-        norm_all = norm_spread
 
         grouped = {}
         pairs = {}
+        flat = {}
         for lo in range(0, COLS, P):
             lead = M if lo == 0 else 0
             grouped[lo] = keep.tile([P, lead + P, PACK], BF16, name=f"grouped{lo}", align_bytes=64)
-        in_place = grouped[384][:, IN_PLACE - 384 :, :]
         for lo, hi in CHUNKS:
             if PLAIN <= lo < IN_PLACE:
-                pairs[lo] = keep.tile([P, 2, hi - lo, 2], BF16, name=f"pairs{lo}", align_bytes=64)
+                flat[lo] = keep.tile([P, 4 * (hi - lo)], BF16, name=f"pairs{lo}", align_bytes=64)
+                pairs[lo] = flat[lo][:].rearrange("p (u n e) -> p u n e", u=2, e=2)
         w_grouped = grouped[0][:, 0:M, :]
         codes = keep.tile([P, M + COLS], U32, name="codes", align_bytes=64)
         scales = keep.tile([P, M + COLS], U8, name="scales", align_bytes=64)
         w_codes, e_codes = codes[:, 0:M], codes[:, M:]
         w_scales, e_scales = scales[:, 0:M], scales[:, M:]
-        picked = [keep.tile([P, COLS], F32, name=f"picked{j}") for j in range(PACK)]
-        summed = [keep.tile([P, COLS], F32, name=f"summed{j}") for j in range(LAST)]
-        rounded = keep.tile([P, 2, COLS], BF16, name="rounded")
-        last_rounded = keep.tile([P, PLAIN], BF16, name="last_rounded")
 
         def words_of(lo, hi):
             first = lo // P * P
             lead = M if first == 0 else 0
             return grouped[first][:, lead + lo - first : lead + hi - first, :]
 
-        tail_sums = keep.tile([P, COLS], F32, name="tail_sums")
-        tail_picked = keep.tile([P, COLS - SHARED], F32, name="tail_picked")
-
-        def sum_of(j, lo, hi):
-            if j < LAST:
-                return summed[j][:, lo:hi]
-            return tail_sums[:, lo:hi]
+        def low_words(lo):
+            return flat[lo][:, 0 : flat[lo].shape[1] // 2].bitcast(F32)
 
         def entries(o, lo, hi):
             first = o * COLS // 16
             return offsets[:, first + lo // 16 : first + hi // 16]
 
-        def pick(o, j):
-            nc.vector.tensor_copy(picked[j][:], windows[o, j].indirect(entries(o, 0, COLS)))
+        def turn(target, source, start=True, stop=True):
+            nc.tensor.matmul(target, source, ident[:], start=start, stop=stop, is_transpose=True)
 
-        def gather(o, j, lo, hi):
+        picked = [keep.tile([P, COLS], F32, name=f"picked{j}") for j in range(PACK)]
+        sums = [psum.tile([P, 2, P], F32, name=f"sums{k}", tag=f"chunk{k}") for k in range(TURNED // P)]
+        own_plane = keep.tile([P, CODEWORDS], F32, name="own_plane")
+        staged = keep.tile([P, HALF], F32, name="staged")
+        once = psum.tile([P, HALF], F32, name="once", tag="chunk3")
+        banked = psum.tile([P, HALF], F32, name="banked")
+
+        def pick(j):
+            window = book0[:, j * CODEWORDS : (j + 1) * CODEWORDS]
+            nc.vector.tensor_copy(picked[j][:], window.indirect(entries(0, 0, COLS)))
+
+        pick(3)
+        for lo in range(0, HALF, P):
+            turn(once[:, lo : lo + P], picked[3][:, HALF + lo : HALF + lo + P])
+        for lo in range(0, CODEWORDS, COLS):
+            nc.scalar.copy(out=own_plane[:, lo : lo + COLS], in_=book0[:, 2 * CODEWORDS + lo : 2 * CODEWORDS + lo + COLS])
+        nc.scalar.copy(out=staged[:], in_=once[:])
+        for lo in range(0, HALF, P):
+            turn(banked[:, lo : lo + P], staged[:, lo : lo + P])
+        nc.scalar.activation(picked[2][:], own_plane[:].indirect(entries(0, 0, COLS)), COPY)
+        for j in range(2):
+            pick(j)
+            for k in range(TURNED // P):
+                turn(sums[k][:, j, :], picked[j][:, k * P : (k + 1) * P], start=(j == 0), stop=False)
+
+        partner = [keep.tile([P, COLS], F32, name=f"partner{j}") for j in range(PACK)]
+        for lo in range(0, COLS, HALF):
+            hi = lo + HALF
+            nc.scalar.activation(partner[0][:, lo:hi], book1_01[:].indirect(entries(1, lo, hi)), COPY)
+            nc.vector.tensor_copy(partner[1][:, lo:hi], book1_01[:, CODEWORDS:].indirect(entries(1, lo, hi)))
+        for k in range(TURNED // P):
+            for j in range(2):
+                turn(sums[k][:, j, :], partner[j][:, k * P : (k + 1) * P], start=False, stop=(j == 1))
+        early = keep.tile([P, 2, COLS - TURNED], F32, name="early")
+        for j in (1, 0):
+            nc.vector.tensor_tensor(early[:, j, :], partner[j][:, TURNED:], picked[j][:, TURNED:], ADD)
+        for lo, hi in CHUNKS[TURNED // P :]:
+            target = pairs[lo][:, 0, :, :] if lo in pairs else words_of(lo, hi)[:, :, 0:2]
             nc.vector.tensor_tensor(
-                sum_of(j, lo, hi), whole[o, j].indirect(entries(o, lo, hi)), picked[j][:, lo:hi], ADD
+                target,
+                early[:, :, lo - TURNED : hi - TURNED].rearrange("p e n -> p n e"),
+                norm_all[:, lo:hi].unsqueeze(2).to_broadcast([P, hi - lo, 2]),
+                MULT,
+            )
+        scaled = [keep.tile([P, P, 2], BF16, name=f"scaled{k}") for k in range(TURNED // P)]
+        back = {}
+
+        def scale(k):
+            source = sums[k][:].rearrange("g e p -> g p e")
+            nc.scalar.activation(scaled[k][:], source, COPY, scale=norm_cols[:, k : k + 1])
+            back[k] = psum.tile([P, P], F32, name=f"back{k}", tag=f"chunk{k}")
+            turn(back[k][:], scaled[k][:].rearrange("g p e -> g (p e)").bitcast(F32))
+
+        def settle(lo, hi):
+            nc.scalar.copy(out=low_words(lo), in_=back[lo // P][:, lo % P : lo % P + hi - lo])
+
+        summed = [keep.tile([P, COLS], F32, name=f"summed{j}") for j in (2, 3)]
+
+        def gather_add(window, j, lo, hi):
+            nc.vector.tensor_tensor(
+                summed[j - 2][:, lo:hi], window[:].indirect(entries(1, lo, hi)), picked[j][:, lo:hi], ADD
             )
 
-        def add(j, lo, hi):
-            if lo >= IN_PLACE:
-                target = in_place[:, :, j]
-            elif lo < PLAIN:
-                target = last_rounded[:, lo:hi] if j == LAST else words_of(lo, hi)[:, :, j]
+        def gather(window, j, lo, hi):
+            nc.scalar.activation(partner[j][:, lo:hi], window[:].indirect(entries(1, lo, hi)), COPY)
+
+        def product(j, lo, hi):
+            if lo in pairs:
+                target = pairs[lo][:, 1, :, j - 2]
             else:
-                target = pairs[lo][:, j // 2, :, j % 2]
-            nc.vector.tensor_tensor(target, sum_of(j, lo, hi), norm_all[:, lo:hi], MULT)
+                target = words_of(lo, hi)[:, :, j]
+            nc.vector.tensor_tensor(target, summed[j - 2][:, lo:hi], norm_all[:, lo:hi], MULT)
 
-        def place(j, lo, hi):
-            nc.scalar.copy(out=words_of(lo, hi)[:, :, j], in_=last_rounded[:, lo:hi])
+        for k in range(TURNED // P):
+            scale(k)
+        lent = {lo + HALF: low_words(lo + P) for lo in range(0, HALF, P)}
+        for lo, target in lent.items():
+            nc.scalar.activation(target, book1_2[:].indirect(entries(1, lo, lo + P)), COPY)
+        gather_add(book1_2, 2, 0, P)
+        gather_add(book1_2, 2, P, HALF)
+        for lo, source in lent.items():
+            nc.vector.tensor_tensor(summed[0][:, lo : lo + P], source, picked[2][:, lo : lo + P], ADD)
+        for chunk in CHUNKS:
+            product(2, *chunk)
+        for chunk in CHUNKS[: TURNED // P]:
+            settle(*chunk)
 
-        def interleave(lo, hi):
-            if lo < PLAIN:
-                place(LAST, lo, hi)
-                return
-            lead = M if lo == 0 else 0
-            words = grouped[lo][:, lead : lead + hi - lo, :].rearrange("p n j -> p (n j)").bitcast(U32)
-            source = pairs[lo][:].rearrange("p u n e -> p u (n e)").bitcast(U32)
-            nc.scalar.copy(out=words.rearrange("p (n u) -> p n u", u=2), in_=source.rearrange("p u n -> p n u"))
-
-        other = keep.tile([P, COLS], F32, name="other")
-        for j in range(LAST):
-            if j == 2:
-                nc.scalar.activation(picked[j][:], whole[0, j].indirect(entries(0, 0, COLS)), COPY)
-            else:
-                pick(0, j)
-            if j == 1:
-                nc.vector.tensor_copy(other[:], windows[1, 1].indirect(entries(1, 0, COLS)))
-                nc.vector.tensor_tensor(summed[j][:], other[:], picked[j][:], ADD)
-            else:
-                gather(1, j, 0, COLS)
-            if j < 2:
-                nc.vector.tensor_tensor(rounded[:, j, :], summed[j][:], norm_all[:], MULT)
-            for lo, hi in CHUNKS:
-                if j == 2:
-                    add(j, lo, hi)
-                if j == 1:
-                    target = pairs[lo][:, 0, :, :] if lo in pairs else words_of(lo, hi)[:, :, 0:2]
-                    nc.scalar.copy(
-                        out=target.rearrange("p (c i) e -> p c e i", i=4),
-                        in_=rounded[:, :, lo:hi].rearrange("p e (c i) -> p c e i", i=4),
-                    )
-        nc.vector.tensor_copy(picked[LAST][:, 0:SHARED], whole[0, LAST].indirect(entries(0, 0, SHARED)))
-        staged = keep.tile([P, COLS], F32, name="staged")
-        banked = psum.tile([P, COLS], F32, name="banked")
-        turned = {}
-        for lo, tag in ((256, "turned"), (384, "y3")):
-            hi = lo + P
-            nc.scalar.activation(picked[LAST][:, lo:hi], whole[0, LAST].indirect(entries(0, lo, hi)), COPY)
-            turned[lo] = psum.tile([P, P], F32, name=f"turned{lo}", tag=tag)
-            nc.tensor.transpose(turned[lo][:], picked[LAST][:, lo:hi], ident[:])
-        nc.scalar.copy(out=staged[:, 256:384], in_=turned[256][:])
-        nc.vector.tensor_copy(out=staged[:, 384:512], in_=turned[384][:])
-        for lo in range(SHARED, COLS, P):
-            nc.tensor.transpose(banked[:, lo : lo + P], staged[:, lo : lo + P], ident[:])
-        for lo in range(SHARED, COLS, P):
-            nc.scalar.activation(
-                tail_picked[:, lo - SHARED : lo - SHARED + P], whole[1, LAST].indirect(entries(1, lo, lo + P)), COPY
-            )
-
+        for lo in range(HALF, COLS, P):
+            gather(book1_3, 3, lo, lo + P)
         nc.gpsimd.tensor_scalar(w_grouped, w_raw[:].rearrange("p j m -> p m j"), 1.0, 0.0, MULT, ADD)
 
         def plain_add(lo):
             nc.vector.tensor_tensor(
-                tail_sums[:, lo : lo + P], tail_picked[:, lo - SHARED : lo - SHARED + P], banked[:, lo : lo + P], ADD
+                summed[1][:, lo : lo + P], partner[3][:, lo : lo + P], banked[:, lo - HALF : lo - HALF + P], ADD
             )
 
+        def interleave(lo, hi):
+            words = words_of(lo, hi).rearrange("p n j -> p (n j)").bitcast(U32)
+            source = flat[lo][:].bitcast(U32).rearrange("p (u n) -> p u n", u=2)
+            nc.scalar.copy(out=words.rearrange("p (n u) -> p n u", u=2), in_=source.rearrange("p u n -> p n u"))
+
         def quantise(lo, hi):
-            source = grouped[lo][:]
             nc.vector.quantize_mx(
                 out=e_codes[:, lo:hi].bitcast(FP8X4),
                 scales=e_scales[:, lo:hi],
-                in_=source.rearrange("p n j -> p (n j)"),
+                in_=words_of(lo, hi).rearrange("p n j -> p (n j)"),
             )
 
         banks = {}
-        for name, lo, hi in (("y0", 0, 128), ("y4", 128, 256), ("y1", 256, 384), ("y2", 384, 448), ("y3", 448, 512)):
-            banks[lo, hi] = psum.tile([P, hi - lo], F32, name=name, tag=name)
+        for (lo, hi), tag in zip(CHUNKS, ("chunk0", "chunk1", "chunk2", "chunk3", "spare")):
+            banks[lo] = psum.tile([P, hi - lo], F32, name=f"bank{lo}", tag=tag)
         result = keep.tile([P, COLS], F32, name="result")
 
         def multiply(lo, hi):
-            for (blo, bhi), bank in banks.items():
-                if blo <= lo and hi <= bhi:
-                    nc.tensor.matmul_mx(
-                        out=bank[:, lo - blo : hi - blo],
-                        lhsT=w_codes.bitcast(FP8X4),
-                        lhsT_scale=w_scales,
-                        rhs=e_codes[:, lo:hi].bitcast(FP8X4),
-                        rhs_scale=e_scales[:, lo:hi],
-                        start=True,
-                        stop=True,
-                    )
+            nc.tensor.matmul_mx(
+                out=banks[lo][:],
+                lhsT=w_codes.bitcast(FP8X4),
+                lhsT_scale=w_scales,
+                rhs=e_codes[:, lo:hi].bitcast(FP8X4),
+                rhs_scale=e_scales[:, lo:hi],
+                start=True,
+                stop=True,
+            )
 
         def evacuate(lo, hi):
-            if lo == 448:
-                nc.vector.tensor_copy(out=result[:, lo:hi], in_=banks[lo, hi][:])
+            if lo == IN_PLACE:
+                nc.vector.tensor_copy(out=result[:, lo:hi], in_=banks[lo][:])
             else:
-                nc.scalar.copy(out=result[:, lo:hi], in_=banks[lo, hi][:])
+                nc.scalar.copy(out=result[:, lo:hi], in_=banks[lo][:])
 
-        def store(queue, lo, hi):
-            queue.dma_start(out=out[:, lo:hi], in_=result[:, lo:hi])
-
-        gather(1, LAST, *CHUNKS[0])
-        gather(1, LAST, *CHUNKS[1])
-        add(LAST, *CHUNKS[0])
+        gather_add(book1_3, 3, *CHUNKS[0])
+        gather_add(book1_3, 3, *CHUNKS[1])
+        product(3, *CHUNKS[0])
         interleave(*CHUNKS[0])
-        add(LAST, *CHUNKS[1])
+        product(3, *CHUNKS[1])
         interleave(*CHUNKS[1])
         plain_add(256)
         plain_add(384)
-        add(LAST, *CHUNKS[2])
+        product(3, *CHUNKS[2])
         interleave(*CHUNKS[2])
-        add(LAST, *CHUNKS[3])
+        product(3, *CHUNKS[3])
         interleave(*CHUNKS[3])
-        add(LAST, *CHUNKS[4])
+        product(3, *CHUNKS[4])
         nc.vector.quantize_mx(
             out=codes[:, 0 : M + P].bitcast(FP8X4),
             scales=scales[:, 0 : M + P],
             in_=grouped[0][:].rearrange("p n j -> p (n j)"),
         )
         multiply(*CHUNKS[0])
-        evacuate(0, 128)
+        evacuate(*CHUNKS[0])
         quantise(*CHUNKS[1])
         multiply(*CHUNKS[1])
-        evacuate(128, 256)
-        store(nc.sync, 0, 256)
+        evacuate(*CHUNKS[1])
+        nc.sync.dma_start(out=out[:, 0:HALF], in_=result[:, 0:HALF])
         quantise(*CHUNKS[2])
         multiply(*CHUNKS[2])
-        evacuate(256, 384)
+        evacuate(*CHUNKS[2])
         quantise(384, COLS)
         multiply(*CHUNKS[3])
         multiply(*CHUNKS[4])
-        evacuate(384, 448)
-        evacuate(448, 512)
-        store(nc.sync, 256, 512)
+        evacuate(*CHUNKS[3])
+        evacuate(*CHUNKS[4])
+        nc.sync.dma_start(out=out[:, HALF:], in_=result[:, HALF:])

@@ -24,8 +24,10 @@ FLOPS = 2 * 512 * COLS * M
 HALF = COLS // 2
 CHUNKS = ((0, 128), (128, 256), (256, 384), (384, 448), (448, 512))
 PLAIN = 0
-IN_PLACE = 448
+IN_PLACE = 480
+WORK = ((0, 128), (128, 256), (256, 384), (384, IN_PLACE), (IN_PLACE, 512))
 TURNED = 384
+SHARED = 192
 
 
 def tile_attend_aq_kernel(tc, cb, w, norm, offs, out):
@@ -46,7 +48,7 @@ def tile_attend_aq_kernel(tc, cb, w, norm, offs, out):
 
         book0 = load_planes(0, 0, 4)
         offsets = keep.tile([P, BOOKS * COLS // 16], U16, name="offsets")
-        nc.sync.dma_start(out=norm_rows[0:4, :], in_=norm[0:1, :].rearrange("o (b j) -> (o b) j", b=4))
+        nc.gpsimd.dma_start(out=norm_rows[0:4, :], in_=norm[0:1, :].rearrange("o (b j) -> (o b) j", b=4))
         nc.sync.dma_start(offsets[:], offs)
         book1_01 = load_planes(1, 0, 2)
         book1_2 = load_planes(1, 2, 1)
@@ -72,7 +74,7 @@ def tile_attend_aq_kernel(tc, cb, w, norm, offs, out):
         for lo in range(0, COLS, P):
             lead = M if lo == 0 else 0
             grouped[lo] = keep.tile([P, lead + P, PACK], BF16, name=f"grouped{lo}", align_bytes=64)
-        for lo, hi in CHUNKS:
+        for lo, hi in WORK:
             if PLAIN <= lo < IN_PLACE:
                 flat[lo] = keep.tile([P, 4 * (hi - lo)], BF16, name=f"pairs{lo}", align_bytes=64)
                 pairs[lo] = flat[lo][:].rearrange("p (u n e) -> p u n e", u=2, e=2)
@@ -100,21 +102,21 @@ def tile_attend_aq_kernel(tc, cb, w, norm, offs, out):
         picked = [keep.tile([P, COLS], F32, name=f"picked{j}") for j in range(PACK)]
         sums = [psum.tile([P, 2, P], F32, name=f"sums{k}", tag=f"chunk{k}") for k in range(TURNED // P)]
         own_plane = keep.tile([P, CODEWORDS], F32, name="own_plane")
-        staged = keep.tile([P, HALF], F32, name="staged")
-        once = psum.tile([P, HALF], F32, name="once", tag="chunk3")
-        banked = psum.tile([P, HALF], F32, name="banked")
+        staged = keep.tile([P, COLS - P], F32, name="staged")
+        once = psum.tile([P, COLS - P], F32, name="once", tag="chunk3")
+        banked = psum.tile([P, COLS - P], F32, name="banked")
 
         def pick(j):
             window = book0[:, j * CODEWORDS : (j + 1) * CODEWORDS]
             nc.vector.tensor_copy(picked[j][:], window.indirect(entries(0, 0, COLS)))
 
         pick(3)
-        for lo in range(0, HALF, P):
-            turn(once[:, lo : lo + P], picked[3][:, HALF + lo : HALF + lo + P])
+        for lo in range(0, COLS - P, P):
+            turn(once[:, lo : lo + P], picked[3][:, P + lo : P + lo + P])
         for lo in range(0, CODEWORDS, COLS):
             nc.scalar.copy(out=own_plane[:, lo : lo + COLS], in_=book0[:, 2 * CODEWORDS + lo : 2 * CODEWORDS + lo + COLS])
         nc.scalar.copy(out=staged[:], in_=once[:])
-        for lo in range(0, HALF, P):
+        for lo in range(0, COLS - P, P):
             turn(banked[:, lo : lo + P], staged[:, lo : lo + P])
         nc.scalar.activation(picked[2][:], own_plane[:].indirect(entries(0, 0, COLS)), COPY)
         for j in range(2):
@@ -123,17 +125,19 @@ def tile_attend_aq_kernel(tc, cb, w, norm, offs, out):
                 turn(sums[k][:, j, :], picked[j][:, k * P : (k + 1) * P], start=(j == 0), stop=False)
 
         partner = [keep.tile([P, COLS], F32, name=f"partner{j}") for j in range(PACK)]
-        for lo in range(0, COLS, HALF):
+        for at in (HALF, 0, TURNED, P):
+            nc.scalar.activation(partner[0][:, at : at + P], book1_01[:].indirect(entries(1, at, at + P)), COPY)
+        for lo in (HALF, 0):
             hi = lo + HALF
-            nc.scalar.activation(partner[0][:, lo:hi], book1_01[:].indirect(entries(1, lo, hi)), COPY)
             nc.vector.tensor_copy(partner[1][:, lo:hi], book1_01[:, CODEWORDS:].indirect(entries(1, lo, hi)))
-        for k in range(TURNED // P):
-            for j in range(2):
-                turn(sums[k][:, j, :], partner[j][:, k * P : (k + 1) * P], start=False, stop=(j == 1))
+        for k in (2, 0, 1):
+            first, second = (1, 0) if k == 1 else (0, 1)
+            turn(sums[k][:, first, :], partner[first][:, k * P : (k + 1) * P], start=False, stop=False)
+            turn(sums[k][:, second, :], partner[second][:, k * P : (k + 1) * P], start=False, stop=True)
         early = keep.tile([P, 2, COLS - TURNED], F32, name="early")
         for j in (1, 0):
             nc.vector.tensor_tensor(early[:, j, :], partner[j][:, TURNED:], picked[j][:, TURNED:], ADD)
-        for lo, hi in CHUNKS[TURNED // P :]:
+        for lo, hi in WORK[TURNED // P :]:
             target = pairs[lo][:, 0, :, :] if lo in pairs else words_of(lo, hi)[:, :, 0:2]
             nc.vector.tensor_tensor(
                 target,
@@ -142,22 +146,22 @@ def tile_attend_aq_kernel(tc, cb, w, norm, offs, out):
                 MULT,
             )
         scaled = [keep.tile([P, P, 2], BF16, name=f"scaled{k}") for k in range(TURNED // P)]
-        back = {}
 
         def scale(k):
             source = sums[k][:].rearrange("g e p -> g p e")
             nc.scalar.activation(scaled[k][:], source, COPY, scale=norm_cols[:, k : k + 1])
-            back[k] = psum.tile([P, P], F32, name=f"back{k}", tag=f"chunk{k}")
-            turn(back[k][:], scaled[k][:].rearrange("g p e -> g (p e)").bitcast(F32))
 
         def settle(lo, hi):
-            nc.scalar.copy(out=low_words(lo), in_=back[lo // P][:, lo % P : lo % P + hi - lo])
+            nc.scalar.copy(out=low_words(lo), in_=back[:, lo:hi])
 
         summed = [keep.tile([P, COLS], F32, name=f"summed{j}") for j in (2, 3)]
 
+        def sum_of(j, lo, hi):
+            return low_words(HALF) if (j, lo) == (2, 0) else summed[j - 2][:, lo:hi]
+
         def gather_add(window, j, lo, hi):
             nc.vector.tensor_tensor(
-                summed[j - 2][:, lo:hi], window[:].indirect(entries(1, lo, hi)), picked[j][:, lo:hi], ADD
+                sum_of(j, lo, hi), window[:].indirect(entries(1, lo, hi)), picked[j][:, lo:hi], ADD
             )
 
         def gather(window, j, lo, hi):
@@ -168,30 +172,33 @@ def tile_attend_aq_kernel(tc, cb, w, norm, offs, out):
                 target = pairs[lo][:, 1, :, j - 2]
             else:
                 target = words_of(lo, hi)[:, :, j]
-            nc.vector.tensor_tensor(target, summed[j - 2][:, lo:hi], norm_all[:, lo:hi], MULT)
+            nc.vector.tensor_tensor(target, sum_of(j, lo, hi), norm_all[:, lo:hi], MULT)
 
-        for k in range(TURNED // P):
+        for k in (2, 0, 1):
             scale(k)
-        lent = {lo + HALF: low_words(lo + P) for lo in range(0, HALF, P)}
-        for lo, target in lent.items():
-            nc.scalar.activation(target, book1_2[:].indirect(entries(1, lo, lo + P)), COPY)
+        back = psum.tile([P, TURNED], F32, name="back", tag="chunk1")
+        for k in range(TURNED // P):
+            turn(back[:, k * P : (k + 1) * P], scaled[k][:].rearrange("g p e -> g (p e)").bitcast(F32))
+        lent = {(lo, lo + P): low_words(lo - HALF) for lo in range(HALF, COLS, P)}
+        for (lo, hi), target in lent.items():
+            nc.scalar.activation(target, book1_2[:].indirect(entries(1, lo, hi)), COPY)
         gather_add(book1_2, 2, 0, P)
         gather_add(book1_2, 2, P, HALF)
-        for lo, source in lent.items():
-            nc.vector.tensor_tensor(summed[0][:, lo : lo + P], source, picked[2][:, lo : lo + P], ADD)
-        for chunk in CHUNKS:
+        for chunk in CHUNKS[:2]:
+            product(2, *chunk)
+        for (lo, hi), source in lent.items():
+            nc.vector.tensor_tensor(summed[0][:, lo:hi], source, picked[2][:, lo:hi], ADD)
+        for chunk in WORK[2:]:
             product(2, *chunk)
         for chunk in CHUNKS[: TURNED // P]:
             settle(*chunk)
 
-        for lo in range(HALF, COLS, P):
-            gather(book1_3, 3, lo, lo + P)
+        for lo, hi in ((SHARED, HALF), (HALF, TURNED), (TURNED, COLS)):
+            gather(book1_3, 3, lo, hi)
         nc.gpsimd.tensor_scalar(w_grouped, w_raw[:].rearrange("p j m -> p m j"), 1.0, 0.0, MULT, ADD)
 
-        def plain_add(lo):
-            nc.vector.tensor_tensor(
-                summed[1][:, lo : lo + P], partner[3][:, lo : lo + P], banked[:, lo - HALF : lo - HALF + P], ADD
-            )
+        def plain_add(lo, hi):
+            nc.vector.tensor_tensor(summed[1][:, lo:hi], partner[3][:, lo:hi], banked[:, lo - P : hi - P], ADD)
 
         def interleave(lo, hi):
             words = words_of(lo, hi).rearrange("p n j -> p (n j)").bitcast(U32)
@@ -222,24 +229,25 @@ def tile_attend_aq_kernel(tc, cb, w, norm, offs, out):
             )
 
         def evacuate(lo, hi):
-            if lo == IN_PLACE:
+            if lo >= HALF:
                 nc.vector.tensor_copy(out=result[:, lo:hi], in_=banks[lo][:])
             else:
                 nc.scalar.copy(out=result[:, lo:hi], in_=banks[lo][:])
 
         gather_add(book1_3, 3, *CHUNKS[0])
-        gather_add(book1_3, 3, *CHUNKS[1])
+        gather_add(book1_3, 3, P, SHARED)
+        plain_add(SHARED, HALF)
         product(3, *CHUNKS[0])
         interleave(*CHUNKS[0])
+        plain_add(HALF, TURNED)
         product(3, *CHUNKS[1])
         interleave(*CHUNKS[1])
-        plain_add(256)
-        plain_add(384)
+        plain_add(TURNED, COLS)
         product(3, *CHUNKS[2])
         interleave(*CHUNKS[2])
-        product(3, *CHUNKS[3])
-        interleave(*CHUNKS[3])
-        product(3, *CHUNKS[4])
+        product(3, *WORK[3])
+        interleave(*WORK[3])
+        product(3, *WORK[4])
         nc.vector.quantize_mx(
             out=codes[:, 0 : M + P].bitcast(FP8X4),
             scales=scales[:, 0 : M + P],

from contextlib import ExitStack

import concourse.mybir as mybir
from concourse.masks import make_identity

F32 = mybir.dt.float32
BF16 = mybir.dt.bfloat16
U32 = mybir.dt.uint32
U16 = mybir.dt.uint16
U8 = mybir.dt.uint8
FP8X4 = mybir.dt.float8_e4m3fn_x4
MULT = mybir.AluOpType.mult
ADD = mybir.AluOpType.add
COPY = mybir.ActivationFunctionType.Copy

P = 128
PACK = 4
BOOKS = 2
CODEWORDS = 2048
COLS = 512
M = 128
FLOPS = 2 * 512 * COLS * M

HALF = COLS // 2
CHUNKS = ((0, 128), (128, 256), (256, 384), (384, 448), (448, 512))
PLAIN = 0
IN_PLACE = 480
WORK = ((0, 128), (128, 256), (256, 384), (384, IN_PLACE), (IN_PLACE, 512))
TURNED = 384
SHARED = 192


def tile_attend_aq_kernel(tc, cb, w, norm, offs, out):
    nc = tc.nc
    with ExitStack() as ctx:
        keep = ctx.enter_context(tc.tile_pool(name="keep", bufs=1))
        psum = ctx.enter_context(tc.psum_pool(name="psum", bufs=1))

        rows = cb.rearrange("o (p j) c -> o p (j c)", j=PACK)

        def load_planes(o, first, count):
            tile = keep.tile([P, count * CODEWORDS], F32, name=f"planes{o}{first}")
            nc.sync.dma_start(out=tile[:], in_=rows[o, :, first * CODEWORDS : (first + count) * CODEWORDS])
            return tile

        norm_rows = keep.tile([P, P], F32, name="norm_rows")
        nc.gpsimd.memset(norm_rows[:], 0.0)

        book0 = load_planes(0, 0, 4)
        offsets = keep.tile([P, BOOKS * COLS // 16], U16, name="offsets")
        nc.gpsimd.dma_start(out=norm_rows[0:4, :], in_=norm[0:1, :].rearrange("o (b j) -> (o b) j", b=4))
        nc.sync.dma_start(offsets[:], offs)
        book1_01 = load_planes(1, 0, 2)
        book1_2 = load_planes(1, 2, 1)
        book1_3 = load_planes(1, 3, 1)
        w_raw = keep.tile([P, PACK, M], F32, name="w_raw")
        nc.sync.dma_start(out=w_raw[:], in_=w.rearrange("(p j) m -> p j m", j=PACK))

        ident = keep.tile([P, P], F32, name="ident")
        make_identity(nc, ident[:])
        norm_turned = psum.tile([P, P], F32, name="norm_turned", tag="spare")
        nc.tensor.transpose(norm_turned[:], norm_rows[:], ident[:])
        norm_cols = keep.tile([P, 4], F32, name="norm_cols")
        nc.scalar.copy(out=norm_cols[:], in_=norm_turned[:, 0:4])
        norm_all = psum.tile([P, COLS], F32, name="norm_all")
        for b in range(4):
            nc.tensor.transpose(
                norm_all[:, b * P : (b + 1) * P], norm_cols[:, b : b + 1].to_broadcast([P, P]), ident[:]
            )

        grouped = {}
        pairs = {}
        flat = {}
        for lo in range(0, COLS, P):
            lead = M if lo == 0 else 0
            grouped[lo] = keep.tile([P, lead + P, PACK], BF16, name=f"grouped{lo}", align_bytes=64)
        for lo, hi in WORK:
            if PLAIN <= lo < IN_PLACE:
                flat[lo] = keep.tile([P, 4 * (hi - lo)], BF16, name=f"pairs{lo}", align_bytes=64)
                pairs[lo] = flat[lo][:].rearrange("p (u n e) -> p u n e", u=2, e=2)
        w_grouped = grouped[0][:, 0:M, :]
        codes = keep.tile([P, M + COLS], U32, name="codes", align_bytes=64)
        scales = keep.tile([P, M + COLS], U8, name="scales", align_bytes=64)
        w_codes, e_codes = codes[:, 0:M], codes[:, M:]
        w_scales, e_scales = scales[:, 0:M], scales[:, M:]

        def words_of(lo, hi):
            first = lo // P * P
            lead = M if first == 0 else 0
            return grouped[first][:, lead + lo - first : lead + hi - first, :]

        def low_words(lo):
            return flat[lo][:, 0 : flat[lo].shape[1] // 2].bitcast(F32)

        def entries(o, lo, hi):
            first = o * COLS // 16
            return offsets[:, first + lo // 16 : first + hi // 16]

        def turn(target, source, start=True, stop=True):
            nc.tensor.matmul(target, source, ident[:], start=start, stop=stop, is_transpose=True)

        picked = [keep.tile([P, COLS], F32, name=f"picked{j}") for j in range(PACK)]
        sums = [psum.tile([P, 2, P], F32, name=f"sums{k}", tag=f"chunk{k}") for k in range(TURNED // P)]
        own_plane = keep.tile([P, CODEWORDS], F32, name="own_plane")
        staged = keep.tile([P, COLS - P], F32, name="staged")
        once = psum.tile([P, COLS - P], F32, name="once", tag="chunk3")
        banked = psum.tile([P, COLS - P], F32, name="banked")

        def pick(j):
            window = book0[:, j * CODEWORDS : (j + 1) * CODEWORDS]
            nc.vector.tensor_copy(picked[j][:], window.indirect(entries(0, 0, COLS)))

        pick(3)
        for lo in range(0, COLS - P, P):
            turn(once[:, lo : lo + P], picked[3][:, P + lo : P + lo + P])
        for lo in range(0, CODEWORDS, COLS):
            nc.scalar.copy(out=own_plane[:, lo : lo + COLS], in_=book0[:, 2 * CODEWORDS + lo : 2 * CODEWORDS + lo + COLS])
        nc.scalar.copy(out=staged[:], in_=once[:])
        for lo in range(0, COLS - P, P):
            turn(banked[:, lo : lo + P], staged[:, lo : lo + P])
        nc.scalar.activation(picked[2][:], own_plane[:].indirect(entries(0, 0, COLS)), COPY)
        for j in range(2):
            pick(j)
            for k in range(TURNED // P):
                turn(sums[k][:, j, :], picked[j][:, k * P : (k + 1) * P], start=(j == 0), stop=False)

        partner = [keep.tile([P, COLS], F32, name=f"partner{j}") for j in range(PACK)]
        for at in (HALF, 0, TURNED, P):
            nc.scalar.activation(partner[0][:, at : at + P], book1_01[:].indirect(entries(1, at, at + P)), COPY)
        for lo in (HALF, 0):
            hi = lo + HALF
            nc.vector.tensor_copy(partner[1][:, lo:hi], book1_01[:, CODEWORDS:].indirect(entries(1, lo, hi)))
        for k in (2, 0, 1):
            first, second = (1, 0) if k == 1 else (0, 1)
            turn(sums[k][:, first, :], partner[first][:, k * P : (k + 1) * P], start=False, stop=False)
            turn(sums[k][:, second, :], partner[second][:, k * P : (k + 1) * P], start=False, stop=True)
        early = keep.tile([P, 2, COLS - TURNED], F32, name="early")
        for j in (1, 0):
            nc.vector.tensor_tensor(early[:, j, :], partner[j][:, TURNED:], picked[j][:, TURNED:], ADD)
        for lo, hi in WORK[TURNED // P :]:
            target = pairs[lo][:, 0, :, :] if lo in pairs else words_of(lo, hi)[:, :, 0:2]
            nc.vector.tensor_tensor(
                target,
                early[:, :, lo - TURNED : hi - TURNED].rearrange("p e n -> p n e"),
                norm_all[:, lo:hi].unsqueeze(2).to_broadcast([P, hi - lo, 2]),
                MULT,
            )
        scaled = [keep.tile([P, P, 2], BF16, name=f"scaled{k}") for k in range(TURNED // P)]

        def scale(k):
            source = sums[k][:].rearrange("g e p -> g p e")
            nc.scalar.activation(scaled[k][:], source, COPY, scale=norm_cols[:, k : k + 1])

        def settle(lo, hi):
            nc.scalar.copy(out=low_words(lo), in_=back[:, lo:hi])

        summed = [keep.tile([P, COLS], F32, name=f"summed{j}") for j in (2, 3)]

        def sum_of(j, lo, hi):
            return low_words(HALF) if (j, lo) == (2, 0) else summed[j - 2][:, lo:hi]

        def gather_add(window, j, lo, hi):
            nc.vector.tensor_tensor(
                sum_of(j, lo, hi), window[:].indirect(entries(1, lo, hi)), picked[j][:, lo:hi], ADD
            )

        def gather(window, j, lo, hi):
            nc.scalar.activation(partner[j][:, lo:hi], window[:].indirect(entries(1, lo, hi)), COPY)

        def product(j, lo, hi):
            if lo in pairs:
                target = pairs[lo][:, 1, :, j - 2]
            else:
                target = words_of(lo, hi)[:, :, j]
            nc.vector.tensor_tensor(target, sum_of(j, lo, hi), norm_all[:, lo:hi], MULT)

        for k in (2, 0, 1):
            scale(k)
        back = psum.tile([P, TURNED], F32, name="back", tag="chunk1")
        for k in range(TURNED // P):
            turn(back[:, k * P : (k + 1) * P], scaled[k][:].rearrange("g p e -> g (p e)").bitcast(F32))
        lent = {(lo, lo + P): low_words(lo - HALF) for lo in range(HALF, COLS, P)}
        for (lo, hi), target in lent.items():
            nc.scalar.activation(target, book1_2[:].indirect(entries(1, lo, hi)), COPY)
        gather_add(book1_2, 2, 0, P)
        gather_add(book1_2, 2, P, HALF)
        for chunk in CHUNKS[:2]:
            product(2, *chunk)
        for (lo, hi), source in lent.items():
            nc.vector.tensor_tensor(summed[0][:, lo:hi], source, picked[2][:, lo:hi], ADD)
        for chunk in WORK[2:]:
            product(2, *chunk)
        for chunk in CHUNKS[: TURNED // P]:
            settle(*chunk)

        for lo, hi in ((SHARED, HALF), (HALF, TURNED), (TURNED, COLS)):
            gather(book1_3, 3, lo, hi)
        nc.gpsimd.tensor_scalar(w_grouped, w_raw[:].rearrange("p j m -> p m j"), 1.0, 0.0, MULT, ADD)

        def plain_add(lo, hi):
            nc.vector.tensor_tensor(summed[1][:, lo:hi], partner[3][:, lo:hi], banked[:, lo - P : hi - P], ADD)

        def interleave(lo, hi):
            words = words_of(lo, hi).rearrange("p n j -> p (n j)").bitcast(U32)
            source = flat[lo][:].bitcast(U32).rearrange("p (u n) -> p u n", u=2)
            nc.scalar.copy(out=words.rearrange("p (n u) -> p n u", u=2), in_=source.rearrange("p u n -> p n u"))

        def quantise(lo, hi):
            nc.vector.quantize_mx(
                out=e_codes[:, lo:hi].bitcast(FP8X4),
                scales=e_scales[:, lo:hi],
                in_=words_of(lo, hi).rearrange("p n j -> p (n j)"),
            )

        banks = {}
        for (lo, hi), tag in zip(CHUNKS, ("chunk0", "chunk1", "chunk2", "chunk3", "spare")):
            banks[lo] = psum.tile([P, hi - lo], F32, name=f"bank{lo}", tag=tag)
        result = keep.tile([P, COLS], F32, name="result")

        def multiply(lo, hi):
            nc.tensor.matmul_mx(
                out=banks[lo][:],
                lhsT=w_codes.bitcast(FP8X4),
                lhsT_scale=w_scales,
                rhs=e_codes[:, lo:hi].bitcast(FP8X4),
                rhs_scale=e_scales[:, lo:hi],
                start=True,
                stop=True,
            )

        def evacuate(lo, hi):
            if lo >= HALF:
                nc.vector.tensor_copy(out=result[:, lo:hi], in_=banks[lo][:])
            else:
                nc.scalar.copy(out=result[:, lo:hi], in_=banks[lo][:])

        gather_add(book1_3, 3, *CHUNKS[0])
        gather_add(book1_3, 3, P, SHARED)
        plain_add(SHARED, HALF)
        product(3, *CHUNKS[0])
        interleave(*CHUNKS[0])
        plain_add(HALF, TURNED)
        product(3, *CHUNKS[1])
        interleave(*CHUNKS[1])
        plain_add(TURNED, COLS)
        product(3, *CHUNKS[2])
        interleave(*CHUNKS[2])
        product(3, *WORK[3])
        interleave(*WORK[3])
        product(3, *WORK[4])
        nc.vector.quantize_mx(
            out=codes[:, 0 : M + P].bitcast(FP8X4),
            scales=scales[:, 0 : M + P],
            in_=grouped[0][:].rearrange("p n j -> p (n j)"),
        )
        multiply(*CHUNKS[0])
        evacuate(*CHUNKS[0])
        quantise(*CHUNKS[1])
        multiply(*CHUNKS[1])
        evacuate(*CHUNKS[1])
        nc.sync.dma_start(out=out[:, 0:HALF], in_=result[:, 0:HALF])
        quantise(*CHUNKS[2])
        multiply(*CHUNKS[2])
        evacuate(*CHUNKS[2])
        quantise(384, COLS)
        multiply(*CHUNKS[3])
        multiply(*CHUNKS[4])
        evacuate(*CHUNKS[3])
        evacuate(*CHUNKS[4])
        nc.sync.dma_start(out=out[:, HALF:], in_=result[:, HALF:])
